import numpy as np
import ml_dtypes


def mxq(x, axis, fmt="e4m3"):
    dtype, down = {"e4m3": (ml_dtypes.float8_e4m3fn, 7), "e5m2": (ml_dtypes.float8_e5m2, 14)}[fmt]
    v = np.moveaxis(np.asarray(x, np.float32).astype(ml_dtypes.bfloat16).astype(np.float64), axis, -1)
    blocks = v.reshape(v.shape[:-1] + (-1, 32))
    amax = np.abs(blocks).max(-1, keepdims=True)
    byte = np.maximum(np.where(amax > 0, np.frexp(amax)[1] - 1 + 127, 0) - down, 1)
    scale = np.exp2(byte - 127.0)
    codes = (blocks / scale).astype(np.float32).astype(dtype).astype(np.float64)
    return np.moveaxis((codes * scale).reshape(v.shape), -1, axis)


WIDE = False


def mx_kscale(k):
    if not WIDE:
        return np.ones(k)
    levels = np.array([24, -24, 12, -12, 0])
    if k % 512:
        return np.exp2(np.random.permutation(np.resize(levels, k // 32))).repeat(32)
    a = np.empty((k // 512, 16))
    for p in range(k // 512):
        a[p, :8] = np.random.permutation(np.resize(levels, 8))
        for g in range(8):
            far = levels[np.abs(levels - a[p, g]) >= 10]
            a[p, g + 8] = far[np.random.randint(len(far))]
    return np.exp2(a.ravel()).repeat(32)


def f64(x):
    return np.asarray(x).astype(np.float64)


def striped(idx):
    return np.tile(idx.reshape(-1, 16).T, (8, 1)).astype(np.uint16)


def unstriped(offs):
    return offs[:16].T.reshape(-1).astype(np.int64)


E2M1 = np.array([0.0, 0.5, 1.0, 1.5, 2.0, 3.0, 4.0, 6.0, -0.0, -0.5, -1.0, -1.5, -2.0, -3.0, -4.0, -6.0])


def pack_weight(w, fmt):
    k, n = w.shape
    w = f64(np.asarray(w, np.float32).astype(ml_dtypes.bfloat16)).reshape(k // 32, 32, n)
    amax = np.abs(w).max(1)
    if fmt == "e4m3":
        byte = np.frexp(amax)[1] - 1 + 127 - 7
    else:
        mant, ex = np.frexp(amax / 6.0)
        byte = np.where(mant > 0.5, ex, ex - 1) + 127
    byte = np.clip(np.where(amax > 0, byte, 1), 1, 254)
    scaled = (w * np.exp2(127.0 - byte)[:, None, :]).reshape(k, n).astype(np.float32)
    by_word = np.ascontiguousarray(scaled.reshape(k // 512, 128, 4, n).transpose(0, 1, 3, 2))
    if fmt == "e4m3":
        words = by_word.astype(ml_dtypes.float8_e4m3fn).view(np.uint8)
    else:
        c = by_word.astype(ml_dtypes.float4_e2m1fn).view(np.uint8) & 0xF
        words = (c[..., 0::2] | (c[..., 1::2] << 4)).reshape(k // 512, 128, 2 * n)
    return np.ascontiguousarray(words), np.ascontiguousarray(byte.astype(np.uint8).reshape(k // 512, 16, n))


def unpack_weight(words, scales, fmt):
    g, _, n = scales.shape
    words = np.ascontiguousarray(words).reshape(g, 128, n, -1)
    if fmt == "e4m3":
        vals = words.view(ml_dtypes.float8_e4m3fn).astype(np.float64)
    else:
        nib = np.empty((g, 128, n, 4), np.uint8)
        nib[..., 0::2] = words & 0xF
        nib[..., 1::2] = words >> 4
        vals = E2M1[nib]
    vals = vals * np.repeat(np.exp2(scales.astype(np.float64) - 127.0), 8, axis=1)[..., None]
    return vals.transpose(0, 1, 3, 2).reshape(g * 512, n)


def pack_table4(v):
    words, scales = pack_weight(v, "e2m1")
    g, t = words.shape[0] // 2, v.shape[1]
    return np.ascontiguousarray(words.reshape(g, 2, 128, t, 2).transpose(0, 2, 3, 1, 4).reshape(g, 128, t, 4)), scales


def unpack_table4(words, scales):
    g, _, t, _ = words.shape
    return unpack_weight(words.reshape(g, 128, t, 2, 2).transpose(0, 3, 1, 2, 4).reshape(2 * g, 128, 2 * t), scales, "e2m1")


def silu(f):
    return f / (1.0 + np.exp(-np.maximum(f, -700.0)))


K, N, T, J = 1024, 1024, 1024, 512


def setup_inputs():
    n = np.random.standard_normal
    s = mx_kscale(K)[:, None]
    wv = n((K, N)) / np.sqrt(K) / s
    p_tab = pack_table4(n((K, T)) * s)
    p_wv4 = pack_weight(wv[512:], "e2m1")
    return {
        "tab_words": p_tab[0],
        "tab_scales": p_tab[1],
        "wk": (n((K, N)) / np.sqrt(K) / s).astype(np.float32),
        "wv8": (wv[:512]).astype(np.float32),
        "wv4_words": p_wv4[0],
        "wv4_scales": p_wv4[1],
        "st": (n((N, J))).astype(np.float32),
        "res": (n((N, J))).astype(np.float32),
        "offs": striped(np.random.permutation(T)[:J]),
    }


def reference(tab_words, tab_scales, wk, wv8, wv4_words, wv4_scales, st, res, offs):
    idx = unstriped(offs)
    tab_ = unpack_table4(tab_words, tab_scales)[:, idx]
    wk_ = mxq(f64(wk), 0, "e4m3")
    wv8_ = mxq(f64(wv8), 0, "e4m3")
    wv4_ = unpack_weight(wv4_words, wv4_scales, "e2m1")
    ke = wk_.T @ tab_
    ve = wv8_.T @ tab_[:512] + wv4_.T @ tab_[512:]
    gate = silu(ke * f64(st))
    return f64(res) + gate * ve

@@ -1,0 +1,190 @@
+from contextlib import ExitStack
+
+import concourse.mybir as mybir
+
+K, N, T, J = 1024, 1024, 1024, 512
+FLOPS = 2 * 2 * K * N * J
+
+F32 = mybir.dt.float32
+BF16 = mybir.dt.bfloat16
+I32 = mybir.dt.int32
+U32 = mybir.dt.uint32
+U16 = mybir.dt.uint16
+U8 = mybir.dt.uint8
+FP8X4 = mybir.dt.float8_e4m3fn_x4
+FP4X4 = mybir.dt.float4_e2m1fn_x4
+MULT = mybir.AluOpType.mult
+ADD = mybir.AluOpType.add
+SILU = mybir.ActivationFunctionType.Silu
+
+P = 128
+PACK = 4
+K_PASS = P * PACK
+HALF = 512
+PIECE = 256
+TILES = N // P
+
+
+def tile_list_engram_qf_silu_kernel(
+    tc, tab_words, tab_scales, wk, wv8, wv4_words, wv4_scales, st, res, offs, out
+):
+    nc = tc.nc
+    with ExitStack() as ctx:
+        keep = ctx.enter_context(tc.tile_pool(name="keep", bufs=1))
+        ring = ctx.enter_context(tc.tile_pool(name="ring", bufs=4))
+        psum = ctx.enter_context(tc.psum_pool(name="psum", bufs=4))
+
+        offsets = keep.tile([P, J // 16], U16, name="offsets")
+        table_words = keep.tile([P, T], I32, name="table_words", align_bytes=64)
+        table_scales = keep.tile([P, 2 * T // 4], I32, name="table_scales", align_bytes=64)
+        wv4_codes = keep.tile([P, 2 * N], U8, name="wv4_codes", align_bytes=64)
+        wv4_plane = keep.tile([P, N // 4], I32, name="wv4_plane", align_bytes=64)
+        warm_in = keep.tile([P, 8], F32, name="warm_in")
+        warm_out = keep.tile([P, 8], F32, name="warm_out")
+
+        nc.vector.memset(table_scales[:], 0)
+        nc.vector.memset(wv4_plane[:], 0)
+        nc.vector.memset(warm_in[:], 0.0)
+        nc.scalar.activation(out=warm_out[:], in_=warm_in[:], func=SILU)
+
+        sources = [wk[0:K_PASS, :], wk[K_PASS:K, :], wv8]
+        raw = {}
+        st_sb = {}
+        res_sb = {}
+
+        def load_weight(w, h):
+            t = keep.tile([P, PACK, HALF], F32, name="raw%d_%d" % (w, h))
+            nc.sync.dma_start(out=t[:], in_=sources[w][:, h * HALF:(h + 1) * HALF].rearrange("(p j) c -> p j c", j=PACK))
+            raw[(w, h)] = t
+
+        def load_rows(src, name, h, into):
+            t = keep.tile([P, 4, J], F32, name="%s%d" % (name, h))
+            nc.sync.dma_start(out=t[:], in_=src[h * HALF:(h + 1) * HALF, :].rearrange("(t p) j -> p t j", p=P))
+            into[h] = t
+
+        nc.sync.dma_start(offsets[:], offs)
+        nc.sync.dma_start(out=table_words[:], in_=tab_words[0].rearrange("p t b -> p (t b)").bitcast(I32))
+        for q in range(4):
+            nc.gpsimd.dma_start(
+                out=table_scales[32 * q:32 * q + 4, :].rearrange("r (a t) -> r a t", a=2),
+                in_=tab_scales[:, 4 * q:4 * q + 4, :].bitcast(I32).rearrange("a r t -> r a t"),
+            )
+        load_weight(0, 0)
+        load_weight(1, 0)
+        nc.sync.dma_start(out=wv4_codes[:].bitcast(I32), in_=wv4_words[0].bitcast(I32))
+        for q in range(4):
+            nc.sync.dma_start(out=wv4_plane[32 * q:32 * q + 4, :], in_=wv4_scales[0, 4 * q:4 * q + 4, :].bitcast(I32))
+        load_weight(2, 0)
+        load_rows(st, "st", 0, st_sb)
+        load_weight(0, 1)
+        load_weight(1, 1)
+        load_rows(st, "st", 1, st_sb)
+        load_rows(res, "res", 0, res_sb)
+        load_weight(2, 1)
+        load_rows(res, "res", 1, res_sb)
+
+        picked_words = keep.tile([P, J], U32, name="picked_words", align_bytes=64)
+        picked_scales = keep.tile([P, 2 * J], U8, name="picked_scales", align_bytes=64)
+        v_codes = keep.tile([P, 2 * 2 * J], U8, name="v_codes", align_bytes=64)
+        nc.vector.tensor_copy(out=picked_words[:], in_=table_words[:].bitcast(U32).indirect(offsets[:]))
+        nc.vector.tensor_copy(
+            out=v_codes[:].bitcast(U16).rearrange("p (d j) -> p d j", d=2),
+            in_=picked_words[:].bitcast(U16).rearrange("p (j d) -> p d j", d=2),
+        )
+        for a in range(2):
+            nc.vector.tensor_copy(
+                out=picked_scales[:, a * J:(a + 1) * J],
+                in_=table_scales[:].bitcast(U8)[:, a * T:(a + 1) * T].indirect(offsets[:]),
+            )
+
+        def v_pass(a):
+            return dict(
+                rhs=v_codes[:, 2 * J * a:2 * J * (a + 1)].bitcast(FP4X4),
+                rhs_scale=picked_scales[:, a * J:(a + 1) * J],
+            )
+
+        codes = [keep.tile([P, N], U32, name="codes%d" % w, align_bytes=64) for w in range(3)]
+        planes = [keep.tile([P, N], U8, name="planes%d" % w, align_bytes=64) for w in range(3)]
+        grouped = {}
+
+        def interleave(w, piece, on_vector):
+            h, c0 = divmod(piece * PIECE, HALF)
+            g = ring.tile([P, PIECE, PACK], BF16, name="grouped", align_bytes=64)
+            dst = g[:].rearrange("p (c i) t -> p c t i", i=4)
+            src = raw[(w, h)][:, :, c0:c0 + PIECE].rearrange("p t (c i) -> p c t i", i=4)
+            if on_vector:
+                nc.vector.tensor_copy(out=dst, in_=src)
+            else:
+                nc.scalar.copy(out=dst, in_=src)
+            grouped[(w, piece)] = g
+
+        def quantize(w, piece):
+            cols = slice(piece * PIECE, (piece + 1) * PIECE)
+            nc.vector.quantize_mx(
+                out=codes[w][:, cols].bitcast(FP8X4),
+                scales=planes[w][:, cols],
+                in_=grouped[(w, piece)][:].rearrange("p c t -> p (c t)"),
+            )
+
+        def weight_pass(w, i):
+            cols = slice(i * P, (i + 1) * P)
+            return dict(lhsT=codes[w][:, cols].bitcast(FP8X4), lhsT_scale=planes[w][:, cols])
+
+        gates = {}
+        gated = {}
+
+        def gate(i):
+            ke = psum.tile([P, J], F32, name="ke")
+            nc.tensor.matmul_mx(out=ke[:], **weight_pass(0, i), **v_pass(0), start=True, stop=False)
+            nc.tensor.matmul_mx(out=ke[:], **weight_pass(1, i), **v_pass(1), start=False, stop=True)
+            f = ring.tile([P, J], F32, name="f")
+            nc.vector.tensor_tensor(out=f[:], in0=ke[:], in1=st_sb[i // 4][:, i % 4, :], op=MULT)
+            g = ring.tile([P, J], F32, name="gate")
+            nc.scalar.activation(out=g[:], in_=f[:], func=SILU)
+            gates[i] = g
+
+        def value(i):
+            ve = psum.tile([P, J], F32, name="ve")
+            nc.tensor.matmul_mx(
+                out=ve[:],
+                lhsT=wv4_codes[:, 2 * P * i:2 * P * (i + 1)].bitcast(FP4X4),
+                lhsT_scale=wv4_plane[:].bitcast(U8)[:, i * P:(i + 1) * P],
+                **v_pass(1),
+                start=True,
+                stop=False,
+            )
+            nc.tensor.matmul_mx(out=ve[:], **weight_pass(2, i), **v_pass(0), start=False, stop=True)
+            gv = keep.tile([P, J], F32, name="gated%d" % i)
+            nc.vector.tensor_tensor(out=gv[:], in0=ve[:], in1=gates[i][:], op=MULT)
+            gated[i] = gv
+
+        def finish(i):
+            o = keep.tile([P, J], F32, name="result%d" % i)
+            nc.vector.tensor_tensor(out=o[:], in0=gated[i][:], in1=res_sb[i // 4][:, i % 4, :], op=ADD)
+            nc.sync.dma_start(out=out[i * P:(i + 1) * P, :], in_=o[:])
+
+        def prepare(w, h, vector_pieces):
+            for piece in (2 * h, 2 * h + 1):
+                interleave(w, piece, piece in vector_pieces)
+            for piece in (2 * h, 2 * h + 1):
+                quantize(w, piece)
+
+        prepare(0, 0, ())
+        prepare(1, 0, ())
+        prepare(2, 0, ())
+        for i in range(4):
+            gate(i)
+        for i in range(4):
+            value(i)
+        prepare(0, 1, ())
+        prepare(1, 1, ())
+        for i in range(4, 8):
+            gate(i)
+        for i in range(4):
+            finish(i)
+        prepare(2, 1, (3,))
+        value(4)
+        for i in range(5, 8):
+            value(i)
+            finish(i - 1)
+        finish(7)

@@ -52,36 +52,41 @@ def tile_list_engram_qf_silu_kernel(
         st_sb = {}
         res_sb = {}
 
-        def load_weight(w, h):
-            t = keep.tile([P, PACK, HALF], F32, name="raw%d_%d" % (w, h))
-            nc.sync.dma_start(out=t[:], in_=sources[w][:, h * HALF:(h + 1) * HALF].rearrange("(p j) c -> p j c", j=PACK))
-            raw[(w, h)] = t
+        def load_weight(w, a, b):
+            t = keep.tile([P, PACK, (b - a) * P], F32, name="raw%d_%d" % (w, a))
+            nc.sync.dma_start(out=t[:], in_=sources[w][:, a * P:b * P].rearrange("(p j) c -> p j c", j=PACK))
+            for i in range(a, b):
+                raw[(w, i)] = (t, a)
 
-        def load_rows(src, name, h, into):
-            t = keep.tile([P, 4, J], F32, name="%s%d" % (name, h))
-            nc.sync.dma_start(out=t[:], in_=src[h * HALF:(h + 1) * HALF, :].rearrange("(t p) j -> p t j", p=P))
-            into[h] = t
+        def load_rows(src, name, a, b, into):
+            t = keep.tile([P, b - a, J], F32, name="%s%d" % (name, a))
+            nc.sync.dma_start(out=t[:], in_=src[a * P:b * P, :].rearrange("(t p) j -> p t j", p=P))
+            for i in range(a, b):
+                into[i] = t[:, i - a, :]
 
         nc.sync.dma_start(offsets[:], offs)
         nc.sync.dma_start(out=table_words[:], in_=tab_words[0].rearrange("p t b -> p (t b)").bitcast(I32))
         for q in range(4):
-            nc.gpsimd.dma_start(
+            nc.sync.dma_start(
                 out=table_scales[32 * q:32 * q + 4, :].rearrange("r (a t) -> r a t", a=2),
                 in_=tab_scales[:, 4 * q:4 * q + 4, :].bitcast(I32).rearrange("a r t -> r a t"),
             )
-        load_weight(0, 0)
-        load_weight(1, 0)
+        load_weight(0, 0, 4)
+        load_weight(1, 0, 4)
+        load_rows(st, "st", 0, 4, st_sb)
         nc.sync.dma_start(out=wv4_codes[:].bitcast(I32), in_=wv4_words[0].bitcast(I32))
         for q in range(4):
             nc.sync.dma_start(out=wv4_plane[32 * q:32 * q + 4, :], in_=wv4_scales[0, 4 * q:4 * q + 4, :].bitcast(I32))
-        load_weight(2, 0)
-        load_rows(st, "st", 0, st_sb)
-        load_weight(0, 1)
-        load_weight(1, 1)
-        load_rows(st, "st", 1, st_sb)
-        load_rows(res, "res", 0, res_sb)
-        load_weight(2, 1)
-        load_rows(res, "res", 1, res_sb)
+        load_weight(2, 0, 4)
+        load_weight(0, 4, 8)
+        load_weight(1, 4, 8)
+        load_weight(2, 4, 8)
+        load_rows(st, "st", 4, 6, st_sb)
+        load_rows(res, "res", 0, 2, res_sb)
+        load_rows(st, "st", 6, 8, st_sb)
+        load_rows(res, "res", 2, 4, res_sb)
+        load_rows(res, "res", 4, 6, res_sb)
+        load_rows(res, "res", 6, 8, res_sb)
 
         picked_words = keep.tile([P, J], U32, name="picked_words", align_bytes=64)
         picked_scales = keep.tile([P, 2 * J], U8, name="picked_scales", align_bytes=64)
@@ -107,23 +112,23 @@ def tile_list_engram_qf_silu_kernel(
         planes = [keep.tile([P, N], U8, name="planes%d" % w, align_bytes=64) for w in range(3)]
         grouped = {}
 
-        def interleave(w, piece, on_vector):
-            h, c0 = divmod(piece * PIECE, HALF)
-            g = ring.tile([P, PIECE, PACK], BF16, name="grouped", align_bytes=64)
+        def interleave(w, a, b, engine):
+            t, first = raw[(w, a)]
+            g = keep.tile([P, (b - a) * P, PACK], BF16, name="grouped%d_%d" % (w, a), align_bytes=64)
             dst = g[:].rearrange("p (c i) t -> p c t i", i=4)
-            src = raw[(w, h)][:, :, c0:c0 + PIECE].rearrange("p t (c i) -> p c t i", i=4)
-            if on_vector:
+            src = t[:, :, (a - first) * P:(b - first) * P].rearrange("p t (c i) -> p c t i", i=4)
+            if engine == "V":
                 nc.vector.tensor_copy(out=dst, in_=src)
             else:
                 nc.scalar.copy(out=dst, in_=src)
-            grouped[(w, piece)] = g
+            grouped[(w, a)] = g
 
-        def quantize(w, piece):
-            cols = slice(piece * PIECE, (piece + 1) * PIECE)
+        def quantize(w, a, b):
+            cols = slice(a * P, b * P)
             nc.vector.quantize_mx(
                 out=codes[w][:, cols].bitcast(FP8X4),
                 scales=planes[w][:, cols],
-                in_=grouped[(w, piece)][:].rearrange("p c t -> p (c t)"),
+                in_=grouped[(w, a)][:].rearrange("p c t -> p (c t)"),
             )
 
         def weight_pass(w, i):
@@ -138,7 +143,7 @@ def tile_list_engram_qf_silu_kernel(
             nc.tensor.matmul_mx(out=ke[:], **weight_pass(0, i), **v_pass(0), start=True, stop=False)
             nc.tensor.matmul_mx(out=ke[:], **weight_pass(1, i), **v_pass(1), start=False, stop=True)
             f = ring.tile([P, J], F32, name="f")
-            nc.vector.tensor_tensor(out=f[:], in0=ke[:], in1=st_sb[i // 4][:, i % 4, :], op=MULT)
+            nc.vector.tensor_tensor(out=f[:], in0=ke[:], in1=st_sb[i], op=MULT)
             g = ring.tile([P, J], F32, name="gate")
             nc.scalar.activation(out=g[:], in_=f[:], func=SILU)
             gates[i] = g
@@ -158,33 +163,73 @@ def tile_list_engram_qf_silu_kernel(
             nc.vector.tensor_tensor(out=gv[:], in0=ve[:], in1=gates[i][:], op=MULT)
             gated[i] = gv
 
-        def finish(i):
-            o = keep.tile([P, J], F32, name="result%d" % i)
-            nc.vector.tensor_tensor(out=o[:], in0=gated[i][:], in1=res_sb[i // 4][:, i % 4, :], op=ADD)
-            nc.sync.dma_start(out=out[i * P:(i + 1) * P, :], in_=o[:])
+        results = {}
+        for group in [[0],[1],[2],[3],[4],[5],[6],[7]]:
+            t = keep.tile([P, len(group), J], F32, name="result%d" % group[0])
+            for i in group:
+                results[i] = t[:, i - group[0], :]
+            results[tuple(group)] = t
 
-        def prepare(w, h, vector_pieces):
-            for piece in (2 * h, 2 * h + 1):
-                interleave(w, piece, piece in vector_pieces)
-            for piece in (2 * h, 2 * h + 1):
-                quantize(w, piece)
+        def finish(i, engine):
+            engine.tensor_tensor(out=results[i], in0=gated[i][:], in1=res_sb[i], op=ADD)
 
-        prepare(0, 0, ())
-        prepare(1, 0, ())
-        prepare(2, 0, ())
-        for i in range(4):
-            gate(i)
-        for i in range(4):
-            value(i)
-        prepare(0, 1, ())
-        prepare(1, 1, ())
-        for i in range(4, 8):
-            gate(i)
-        for i in range(4):
-            finish(i)
-        prepare(2, 1, (3,))
+        def store(*group):
+            rows = out[group[0] * P:(group[-1] + 1) * P, :]
+            nc.sync.dma_start(out=rows.rearrange("(t p) j -> p t j", p=P), in_=results[group][:])
+
+        interleave(0, 0, 2, "S")
+        interleave(0, 2, 4, "S")
+        quantize(0, 0, 2)
+        quantize(0, 2, 4)
+        interleave(1, 0, 2, "S")
+        interleave(1, 2, 4, "S")
+        quantize(1, 0, 2)
+        quantize(1, 2, 4)
+        gate(0)
+        gate(1)
+        gate(2)
+        gate(3)
+        interleave(2, 0, 2, "V")
+        interleave(2, 2, 4, "S")
+        quantize(2, 0, 2)
+        quantize(2, 2, 4)
+        value(0)
+        value(1)
+        value(2)
+        value(3)
+        interleave(0, 4, 6, "S")
+        interleave(0, 6, 8, "S")
+        quantize(0, 4, 6)
+        quantize(0, 6, 8)
+        interleave(1, 4, 6, "V")
+        interleave(1, 6, 8, "S")
+        quantize(1, 4, 6)
+        quantize(1, 6, 8)
+        interleave(2, 4, 6, "V")
+        interleave(2, 6, 8, "S")
+        quantize(2, 4, 6)
+        quantize(2, 6, 8)
+        gate(4)
+        gate(5)
         value(4)
-        for i in range(5, 8):
-            value(i)
-            finish(i - 1)
-        finish(7)
+        value(5)
+        finish(0, nc.gpsimd)
+        store(0)
+        finish(1, nc.gpsimd)
+        store(1)
+        gate(6)
+        gate(7)
+        value(6)
+        value(7)
+        finish(2, nc.gpsimd)
+        store(2)
+        finish(3, nc.gpsimd)
+        store(3)
+        finish(4, nc.vector)
+        store(4)
+        finish(5, nc.vector)
+        store(5)
+        finish(6, nc.vector)
+        store(6)
+        finish(7, nc.vector)
+        store(7)

@@ -68,23 +68,23 @@ def tile_list_engram_qf_silu_kernel(
         nc.sync.dma_start(out=table_words[:], in_=tab_words[0].rearrange("p t b -> p (t b)").bitcast(I32))
         for q in range(4):
             nc.sync.dma_start(
-                out=table_scales[32 * q:32 * q + 4, :].rearrange("r (a t) -> r a t", a=2),
-                in_=tab_scales[:, 4 * q:4 * q + 4, :].bitcast(I32).rearrange("a r t -> r a t"),
+                out=table_scales[q:P:32, :].rearrange("r (a t) -> r a t", a=2),
+                in_=tab_scales[:, q:16:4, :].bitcast(I32).rearrange("a r t -> r a t"),
             )
         load_weight(0, 0, 4)
         load_weight(1, 0, 4)
+        load_weight(2, 0, 4)
         load_rows(st, "st", 0, 4, st_sb)
         nc.sync.dma_start(out=wv4_codes[:].bitcast(I32), in_=wv4_words[0].bitcast(I32))
         for q in range(4):
-            nc.sync.dma_start(out=wv4_plane[32 * q:32 * q + 4, :], in_=wv4_scales[0, 4 * q:4 * q + 4, :].bitcast(I32))
-        load_weight(2, 0, 4)
+            nc.sync.dma_start(out=wv4_plane[q:P:32, :], in_=wv4_scales[0, q:16:4, :].bitcast(I32))
         load_weight(0, 4, 8)
         load_weight(1, 4, 8)
         load_weight(2, 4, 8)
-        load_rows(st, "st", 4, 6, st_sb)
         load_rows(res, "res", 0, 2, res_sb)
-        load_rows(st, "st", 6, 8, st_sb)
+        load_rows(st, "st", 4, 6, st_sb)
         load_rows(res, "res", 2, 4, res_sb)
+        load_rows(st, "st", 6, 8, st_sb)
         load_rows(res, "res", 4, 6, res_sb)
         load_rows(res, "res", 6, 8, res_sb)
 
@@ -185,19 +185,19 @@ def tile_list_engram_qf_silu_kernel(
         interleave(1, 2, 4, "S")
         quantize(1, 0, 2)
         quantize(1, 2, 4)
-        gate(0)
-        gate(1)
-        gate(2)
-        gate(3)
         interleave(2, 0, 2, "V")
         interleave(2, 2, 4, "S")
         quantize(2, 0, 2)
         quantize(2, 2, 4)
+        gate(0)
+        gate(1)
         value(0)
         value(1)
+        gate(2)
+        gate(3)
         value(2)
         value(3)
-        interleave(0, 4, 6, "S")
+        interleave(0, 4, 6, "V")
         interleave(0, 6, 8, "S")
         quantize(0, 4, 6)
         quantize(0, 6, 8)
@@ -205,27 +205,27 @@ def tile_list_engram_qf_silu_kernel(
         interleave(1, 6, 8, "S")
         quantize(1, 4, 6)
         quantize(1, 6, 8)
-        interleave(2, 4, 6, "V")
+        interleave(2, 4, 6, "S")
         interleave(2, 6, 8, "S")
         quantize(2, 4, 6)
         quantize(2, 6, 8)
+        finish(0, nc.vector)
+        store(0)
+        finish(1, nc.vector)
+        store(1)
         gate(4)
         gate(5)
         value(4)
         value(5)
-        finish(0, nc.gpsimd)
-        store(0)
-        finish(1, nc.gpsimd)
-        store(1)
-        gate(6)
-        gate(7)
-        value(6)
-        value(7)
         finish(2, nc.gpsimd)
         store(2)
         finish(3, nc.gpsimd)
         store(3)
-        finish(4, nc.vector)
+        gate(6)
+        gate(7)
+        value(6)
+        value(7)
+        finish(4, nc.gpsimd)
         store(4)
         finish(5, nc.vector)
         store(5)

@@ -71,14 +71,13 @@ def tile_list_engram_qf_silu_kernel(
                 out=table_scales[q:P:32, :].rearrange("r (a t) -> r a t", a=2),
                 in_=tab_scales[:, q:16:4, :].bitcast(I32).rearrange("a r t -> r a t"),
             )
-        load_weight(0, 0, 4)
+        load_weight(0, 0, 8)
         load_weight(1, 0, 4)
         load_weight(2, 0, 4)
         load_rows(st, "st", 0, 4, st_sb)
         nc.sync.dma_start(out=wv4_codes[:].bitcast(I32), in_=wv4_words[0].bitcast(I32))
         for q in range(4):
             nc.sync.dma_start(out=wv4_plane[q:P:32, :], in_=wv4_scales[0, q:16:4, :].bitcast(I32))
-        load_weight(0, 4, 8)
         load_weight(1, 4, 8)
         load_weight(2, 4, 8)
         load_rows(res, "res", 0, 2, res_sb)
@@ -177,11 +176,15 @@ def tile_list_engram_qf_silu_kernel(
             rows = out[group[0] * P:(group[-1] + 1) * P, :]
             nc.sync.dma_start(out=rows.rearrange("(t p) j -> p t j", p=P), in_=results[group][:])
 
-        interleave(0, 0, 2, "S")
+        interleave(0, 0, 2, "V")
         interleave(0, 2, 4, "S")
+        interleave(0, 4, 6, "V")
+        interleave(0, 6, 8, "S")
         quantize(0, 0, 2)
         quantize(0, 2, 4)
-        interleave(1, 0, 2, "S")
+        quantize(0, 4, 6)
+        quantize(0, 6, 8)
+        interleave(1, 0, 2, "V")
         interleave(1, 2, 4, "S")
         quantize(1, 0, 2)
         quantize(1, 2, 4)
@@ -197,11 +200,7 @@ def tile_list_engram_qf_silu_kernel(
         gate(3)
         value(2)
         value(3)
-        interleave(0, 4, 6, "V")
-        interleave(0, 6, 8, "S")
-        quantize(0, 4, 6)
-        quantize(0, 6, 8)
-        interleave(1, 4, 6, "V")
+        interleave(1, 4, 6, "S")
         interleave(1, 6, 8, "S")
         quantize(1, 4, 6)
         quantize(1, 6, 8)

@@ -64,26 +64,31 @@ def tile_list_engram_qf_silu_kernel(
             for i in range(a, b):
                 into[i] = t[:, i - a, :]
 
-        nc.sync.dma_start(offsets[:], offs)
+        def load_scale_rows(plane, rows, passes):
+            for r in range(4):
+                nc.sync.dma_start(
+                    out=plane[r:P:32, :].rearrange("q (a t) -> q a t", a=passes),
+                    in_=rows[:, r:16:4, :].bitcast(I32).rearrange("a q t -> q a t"),
+                )
+
+        def load_wv4():
+            nc.sync.dma_start(out=wv4_codes[:].bitcast(I32), in_=wv4_words[0].bitcast(I32))
+            load_scale_rows(wv4_plane, wv4_scales, 1)
+
         nc.sync.dma_start(out=table_words[:], in_=tab_words[0].rearrange("p t b -> p (t b)").bitcast(I32))
-        for q in range(4):
-            nc.sync.dma_start(
-                out=table_scales[q:P:32, :].rearrange("r (a t) -> r a t", a=2),
-                in_=tab_scales[:, q:16:4, :].bitcast(I32).rearrange("a r t -> r a t"),
-            )
+        nc.sync.dma_start(offsets[:], offs)
+        load_scale_rows(table_scales, tab_scales, 2)
         load_weight(0, 0, 8)
         load_weight(1, 0, 4)
-        load_weight(2, 0, 4)
         load_rows(st, "st", 0, 4, st_sb)
-        nc.sync.dma_start(out=wv4_codes[:].bitcast(I32), in_=wv4_words[0].bitcast(I32))
-        for q in range(4):
-            nc.sync.dma_start(out=wv4_plane[q:P:32, :], in_=wv4_scales[0, q:16:4, :].bitcast(I32))
         load_weight(1, 4, 8)
+        load_weight(2, 0, 4)
         load_weight(2, 4, 8)
+        load_wv4()
         load_rows(res, "res", 0, 2, res_sb)
         load_rows(st, "st", 4, 6, st_sb)
-        load_rows(res, "res", 2, 4, res_sb)
         load_rows(st, "st", 6, 8, st_sb)
+        load_rows(res, "res", 2, 4, res_sb)
         load_rows(res, "res", 4, 6, res_sb)
         load_rows(res, "res", 6, 8, res_sb)
 
@@ -137,98 +142,67 @@ def tile_list_engram_qf_silu_kernel(
         gates = {}
         gated = {}
 
-        def gate(i):
+        keys = {}
+        values = {}
+
+        def key(i):
             ke = psum.tile([P, J], F32, name="ke")
             nc.tensor.matmul_mx(out=ke[:], **weight_pass(0, i), **v_pass(0), start=True, stop=False)
             nc.tensor.matmul_mx(out=ke[:], **weight_pass(1, i), **v_pass(1), start=False, stop=True)
+            keys[i] = ke
+
+        def gate(i):
             f = ring.tile([P, J], F32, name="f")
-            nc.vector.tensor_tensor(out=f[:], in0=ke[:], in1=st_sb[i], op=MULT)
-            g = ring.tile([P, J], F32, name="gate")
+            nc.vector.tensor_tensor(out=f[:], in0=keys[i][:], in1=st_sb[i], op=MULT)
+            g = keep.tile([P, J], F32, name="gate%d" % i, tag="late" if i == TILES - 1 else "gate%d" % i)
             nc.scalar.activation(out=g[:], in_=f[:], func=SILU)
             gates[i] = g
 
         def value(i):
             ve = psum.tile([P, J], F32, name="ve")
-            nc.tensor.matmul_mx(
-                out=ve[:],
+            wv4_pass = dict(
                 lhsT=wv4_codes[:, 2 * P * i:2 * P * (i + 1)].bitcast(FP4X4),
                 lhsT_scale=wv4_plane[:].bitcast(U8)[:, i * P:(i + 1) * P],
-                **v_pass(1),
-                start=True,
-                stop=False,
             )
-            nc.tensor.matmul_mx(out=ve[:], **weight_pass(2, i), **v_pass(0), start=False, stop=True)
+            nc.tensor.matmul_mx(out=ve[:], **weight_pass(2, i), **v_pass(0), start=True, stop=False)
+            nc.tensor.matmul_mx(out=ve[:], **wv4_pass, **v_pass(1), start=False, stop=True)
+            values[i] = ve
+
+        def let_through(i):
             gv = keep.tile([P, J], F32, name="gated%d" % i)
-            nc.vector.tensor_tensor(out=gv[:], in0=ve[:], in1=gates[i][:], op=MULT)
+            nc.vector.tensor_tensor(out=gv[:], in0=values[i][:], in1=gates[i][:], op=MULT)
             gated[i] = gv
 
-        results = {}
-        for group in [[0],[1],[2],[3],[4],[5],[6],[7]]:
-            t = keep.tile([P, len(group), J], F32, name="result%d" % group[0])
-            for i in group:
-                results[i] = t[:, i - group[0], :]
-            results[tuple(group)] = t
+        def finish(a, b, engine, tag, group, align):
+            t = keep.tile([P, b - a, J], F32, name="result%d" % a, tag=tag, align_bytes=align)
+            for i in range(a, b):
+                engine.tensor_tensor(out=t[:, i - a, :], in0=gated[i][:], in1=res_sb[i], op=ADD)
+                if (i - a + 1) % group == 0:
+                    s = i + 1 - group
+                    rows = out[s * P:(i + 1) * P, :].rearrange("(t p) j -> p t j", p=P)
+                    nc.sync.dma_start(out=rows, in_=t[:, s - a:i + 1 - a, :])
 
-        def finish(i, engine):
-            engine.tensor_tensor(out=results[i], in0=gated[i][:], in1=res_sb[i], op=ADD)
+        def prepare(w, a, b):
+            for c in range(a, b, 4):
+                interleave(w, c, c + 2, "V")
+                interleave(w, c + 2, c + 4, "S")
+            for c in range(a, b, 2):
+                quantize(w, c, c + 2)
 
-        def store(*group):
-            rows = out[group[0] * P:(group[-1] + 1) * P, :]
-            nc.sync.dma_start(out=rows.rearrange("(t p) j -> p t j", p=P), in_=results[group][:])
-
-        interleave(0, 0, 2, "V")
-        interleave(0, 2, 4, "S")
-        interleave(0, 4, 6, "V")
-        interleave(0, 6, 8, "S")
-        quantize(0, 0, 2)
-        quantize(0, 2, 4)
-        quantize(0, 4, 6)
-        quantize(0, 6, 8)
-        interleave(1, 0, 2, "V")
-        interleave(1, 2, 4, "S")
-        quantize(1, 0, 2)
-        quantize(1, 2, 4)
-        interleave(2, 0, 2, "V")
-        interleave(2, 2, 4, "S")
-        quantize(2, 0, 2)
-        quantize(2, 2, 4)
-        gate(0)
-        gate(1)
-        value(0)
-        value(1)
-        gate(2)
-        gate(3)
-        value(2)
-        value(3)
-        interleave(1, 4, 6, "S")
-        interleave(1, 6, 8, "S")
-        quantize(1, 4, 6)
-        quantize(1, 6, 8)
-        interleave(2, 4, 6, "S")
-        interleave(2, 6, 8, "S")
-        quantize(2, 4, 6)
-        quantize(2, 6, 8)
-        finish(0, nc.vector)
-        store(0)
-        finish(1, nc.vector)
-        store(1)
-        gate(4)
-        gate(5)
-        value(4)
-        value(5)
-        finish(2, nc.gpsimd)
-        store(2)
-        finish(3, nc.gpsimd)
-        store(3)
-        gate(6)
-        gate(7)
-        value(6)
-        value(7)
-        finish(4, nc.gpsimd)
-        store(4)
-        finish(5, nc.vector)
-        store(5)
-        finish(6, nc.vector)
-        store(6)
-        finish(7, nc.vector)
-        store(7)
+        prepare(0, 0, 8)
+        prepare(1, 0, 4)
+        for i in range(4):
+            key(i)
+            gate(i)
+        prepare(1, 4, 8)
+        for i in range(4, 8):
+            key(i)
+        prepare(2, 0, 4)
+        prepare(2, 4, 8)
+        for i in range(4, 8):
+            gate(i)
+        for i in range(8):
+            value(i)
+            let_through(i)
+        finish(0, 4, nc.gpsimd, "grouped2_6", 1, 64)
+        finish(4, 8, nc.vector, "late", 1, 32)

@@ -79,9 +79,8 @@ def tile_list_engram_qf_silu_kernel(
         nc.sync.dma_start(offsets[:], offs)
         load_scale_rows(table_scales, tab_scales, 2)
         load_weight(0, 0, 8)
-        load_weight(1, 0, 4)
+        load_weight(1, 0, 8)
         load_rows(st, "st", 0, 4, st_sb)
-        load_weight(1, 4, 8)
         load_weight(2, 0, 4)
         load_weight(2, 4, 8)
         load_wv4()
@@ -190,16 +189,14 @@ def tile_list_engram_qf_silu_kernel(
                 quantize(w, c, c + 2)
 
         prepare(0, 0, 8)
-        prepare(1, 0, 4)
+        prepare(1, 0, 8)
         for i in range(4):
             key(i)
             gate(i)
-        prepare(1, 4, 8)
-        for i in range(4, 8):
-            key(i)
         prepare(2, 0, 4)
         prepare(2, 4, 8)
         for i in range(4, 8):
+            key(i)
             gate(i)
         for i in range(8):
             value(i)

@@ -71,23 +71,20 @@ def tile_list_engram_qf_silu_kernel(
                     in_=rows[:, r:16:4, :].bitcast(I32).rearrange("a q t -> q a t"),
                 )
 
-        def load_wv4():
-            nc.sync.dma_start(out=wv4_codes[:].bitcast(I32), in_=wv4_words[0].bitcast(I32))
-            load_scale_rows(wv4_plane, wv4_scales, 1)
-
         nc.sync.dma_start(out=table_words[:], in_=tab_words[0].rearrange("p t b -> p (t b)").bitcast(I32))
         nc.sync.dma_start(offsets[:], offs)
         load_scale_rows(table_scales, tab_scales, 2)
         load_weight(0, 0, 8)
+        load_scale_rows(wv4_plane, wv4_scales, 1)
         load_weight(1, 0, 8)
-        load_rows(st, "st", 0, 4, st_sb)
-        load_weight(2, 0, 4)
-        load_weight(2, 4, 8)
-        load_wv4()
+        load_weight(2, 0, 8)
+        load_rows(st, "st", 0, 2, st_sb)
+        nc.sync.dma_start(out=wv4_codes[:].bitcast(I32), in_=wv4_words[0].bitcast(I32))
+        load_rows(st, "st", 2, 4, st_sb)
         load_rows(res, "res", 0, 2, res_sb)
         load_rows(st, "st", 4, 6, st_sb)
-        load_rows(st, "st", 6, 8, st_sb)
         load_rows(res, "res", 2, 4, res_sb)
+        load_rows(st, "st", 6, 8, st_sb)
         load_rows(res, "res", 4, 6, res_sb)
         load_rows(res, "res", 6, 8, res_sb)
 
@@ -163,8 +160,8 @@ def tile_list_engram_qf_silu_kernel(
                 lhsT=wv4_codes[:, 2 * P * i:2 * P * (i + 1)].bitcast(FP4X4),
                 lhsT_scale=wv4_plane[:].bitcast(U8)[:, i * P:(i + 1) * P],
             )
-            nc.tensor.matmul_mx(out=ve[:], **weight_pass(2, i), **v_pass(0), start=True, stop=False)
-            nc.tensor.matmul_mx(out=ve[:], **wv4_pass, **v_pass(1), start=False, stop=True)
+            nc.tensor.matmul_mx(out=ve[:], **wv4_pass, **v_pass(1), start=True, stop=False)
+            nc.tensor.matmul_mx(out=ve[:], **weight_pass(2, i), **v_pass(0), start=False, stop=True)
             values[i] = ve
 
         def let_through(i):
@@ -181,25 +178,24 @@ def tile_list_engram_qf_silu_kernel(
                     rows = out[s * P:(i + 1) * P, :].rearrange("(t p) j -> p t j", p=P)
                     nc.sync.dma_start(out=rows, in_=t[:, s - a:i + 1 - a, :])
 
-        def prepare(w, a, b):
-            for c in range(a, b, 4):
+        def prepare(w):
+            for c in range(0, TILES, 4):
                 interleave(w, c, c + 2, "V")
                 interleave(w, c + 2, c + 4, "S")
-            for c in range(a, b, 2):
+            for c in range(0, TILES, 2):
                 quantize(w, c, c + 2)
 
-        prepare(0, 0, 8)
-        prepare(1, 0, 8)
-        for i in range(4):
+        prepare(0)
+        prepare(1)
+        prepare(2)
+        for i in range(0, 3):
             key(i)
             gate(i)
-        prepare(2, 0, 4)
-        prepare(2, 4, 8)
-        for i in range(4, 8):
-            key(i)
-            gate(i)
-        for i in range(8):
+        for i in range(TILES):
             value(i)
             let_through(i)
-        finish(0, 4, nc.gpsimd, "grouped2_6", 1, 64)
-        finish(4, 8, nc.vector, "late", 1, 32)
+            if i + 3 < TILES:
+                key(i + 3)
+                gate(i + 3)
+        finish(0, 5, nc.gpsimd, "grouped2_6", 1, 64)
+        finish(5, 8, nc.vector, "late", 1, 32)

@@ -81,12 +81,12 @@ def tile_list_engram_qf_silu_kernel(
         load_rows(st, "st", 0, 2, st_sb)
         nc.sync.dma_start(out=wv4_codes[:].bitcast(I32), in_=wv4_words[0].bitcast(I32))
         load_rows(st, "st", 2, 4, st_sb)
-        load_rows(res, "res", 0, 2, res_sb)
+        load_rows(res, "res", 0, 1, res_sb)
         load_rows(st, "st", 4, 6, st_sb)
-        load_rows(res, "res", 2, 4, res_sb)
+        load_rows(res, "res", 1, 3, res_sb)
         load_rows(st, "st", 6, 8, st_sb)
-        load_rows(res, "res", 4, 6, res_sb)
-        load_rows(res, "res", 6, 8, res_sb)
+        load_rows(res, "res", 3, 5, res_sb)
+        load_rows(res, "res", 5, 8, res_sb)
 
         picked_words = keep.tile([P, J], U32, name="picked_words", align_bytes=64)
         picked_scales = keep.tile([P, 2 * J], U8, name="picked_scales", align_bytes=64)
@@ -142,7 +142,7 @@ def tile_list_engram_qf_silu_kernel(
         values = {}
 
         def key(i):
-            ke = psum.tile([P, J], F32, name="ke")
+            ke = psum.tile([P, J], F32, name="ke", bufs=5)
             nc.tensor.matmul_mx(out=ke[:], **weight_pass(0, i), **v_pass(0), start=True, stop=False)
             nc.tensor.matmul_mx(out=ke[:], **weight_pass(1, i), **v_pass(1), start=False, stop=True)
             keys[i] = ke
@@ -155,7 +155,7 @@ def tile_list_engram_qf_silu_kernel(
             gates[i] = g
 
         def value(i):
-            ve = psum.tile([P, J], F32, name="ve")
+            ve = psum.tile([P, J], F32, name="ve", bufs=3)
             wv4_pass = dict(
                 lhsT=wv4_codes[:, 2 * P * i:2 * P * (i + 1)].bitcast(FP4X4),
                 lhsT_scale=wv4_plane[:].bitcast(U8)[:, i * P:(i + 1) * P],

@@ -150,7 +150,7 @@ def tile_list_engram_qf_silu_kernel(
         def gate(i):
             f = ring.tile([P, J], F32, name="f")
             nc.vector.tensor_tensor(out=f[:], in0=keys[i][:], in1=st_sb[i], op=MULT)
-            g = keep.tile([P, J], F32, name="gate%d" % i, tag="late" if i == TILES - 1 else "gate%d" % i)
+            g = keep.tile([P, J], F32, name="gate%d" % i, tag="late" if i == TILES - 2 else "gate%d" % i)
             nc.scalar.activation(out=g[:], in_=f[:], func=SILU)
             gates[i] = g
 

@@ -81,11 +81,12 @@ def tile_list_engram_qf_silu_kernel(
         load_rows(st, "st", 0, 2, st_sb)
         nc.sync.dma_start(out=wv4_codes[:].bitcast(I32), in_=wv4_words[0].bitcast(I32))
         load_rows(st, "st", 2, 4, st_sb)
-        load_rows(res, "res", 0, 1, res_sb)
+        load_rows(res, "res", 0, 2, res_sb)
         load_rows(st, "st", 4, 6, st_sb)
-        load_rows(res, "res", 1, 3, res_sb)
+        load_rows(res, "res", 2, 3, res_sb)
         load_rows(st, "st", 6, 8, st_sb)
-        load_rows(res, "res", 3, 5, res_sb)
+        load_rows(res, "res", 3, 4, res_sb)
+        load_rows(res, "res", 4, 5, res_sb)
         load_rows(res, "res", 5, 8, res_sb)
 
         picked_words = keep.tile([P, J], U32, name="picked_words", align_bytes=64)

@@ -38,12 +38,10 @@ def tile_list_engram_qf_silu_kernel(
         table_words = keep.tile([P, T], I32, name="table_words", align_bytes=64)
         table_scales = keep.tile([P, 2 * T // 4], I32, name="table_scales", align_bytes=64)
         wv4_codes = keep.tile([P, 2 * N], U8, name="wv4_codes", align_bytes=64)
-        wv4_plane = keep.tile([P, N // 4], I32, name="wv4_plane", align_bytes=64)
         warm_in = keep.tile([P, 8], F32, name="warm_in")
         warm_out = keep.tile([P, 8], F32, name="warm_out")
 
         nc.vector.memset(table_scales[:], 0)
-        nc.vector.memset(wv4_plane[:], 0)
         nc.vector.memset(warm_in[:], 0.0)
         nc.scalar.activation(out=warm_out[:], in_=warm_in[:], func=SILU)
 
@@ -58,36 +56,28 @@ def tile_list_engram_qf_silu_kernel(
             for i in range(a, b):
                 raw[(w, i)] = (t, a)
 
-        def load_rows(src, name, a, b, into):
-            t = keep.tile([P, b - a, J], F32, name="%s%d" % (name, a))
+        def load_rows(src, name, a, b, into, tag=None):
+            t = keep.tile([P, b - a, J], F32, name="%s%d" % (name, a), tag=tag or "%s%d" % (name, a), align_bytes=64)
             nc.sync.dma_start(out=t[:], in_=src[a * P:b * P, :].rearrange("(t p) j -> p t j", p=P))
             for i in range(a, b):
                 into[i] = t[:, i - a, :]
 
-        def load_scale_rows(plane, rows, passes):
+        def load_scale_rows(queue, plane, rows, passes):
             for r in range(4):
-                nc.sync.dma_start(
+                queue.dma_start(
                     out=plane[r:P:32, :].rearrange("q (a t) -> q a t", a=passes),
                     in_=rows[:, r:16:4, :].bitcast(I32).rearrange("a q t -> q a t"),
                 )
 
         nc.sync.dma_start(out=table_words[:], in_=tab_words[0].rearrange("p t b -> p (t b)").bitcast(I32))
         nc.sync.dma_start(offsets[:], offs)
-        load_scale_rows(table_scales, tab_scales, 2)
+        load_scale_rows(nc.sync, table_scales, tab_scales, 2)
         load_weight(0, 0, 8)
-        load_scale_rows(wv4_plane, wv4_scales, 1)
         load_weight(1, 0, 8)
         load_weight(2, 0, 8)
         load_rows(st, "st", 0, 2, st_sb)
         nc.sync.dma_start(out=wv4_codes[:].bitcast(I32), in_=wv4_words[0].bitcast(I32))
         load_rows(st, "st", 2, 4, st_sb)
-        load_rows(res, "res", 0, 2, res_sb)
-        load_rows(st, "st", 4, 6, st_sb)
-        load_rows(res, "res", 2, 3, res_sb)
-        load_rows(st, "st", 6, 8, st_sb)
-        load_rows(res, "res", 3, 4, res_sb)
-        load_rows(res, "res", 4, 5, res_sb)
-        load_rows(res, "res", 5, 8, res_sb)
 
         picked_words = keep.tile([P, J], U32, name="picked_words", align_bytes=64)
         picked_scales = keep.tile([P, 2 * J], U8, name="picked_scales", align_bytes=64)
@@ -161,8 +151,8 @@ def tile_list_engram_qf_silu_kernel(
                 lhsT=wv4_codes[:, 2 * P * i:2 * P * (i + 1)].bitcast(FP4X4),
                 lhsT_scale=wv4_plane[:].bitcast(U8)[:, i * P:(i + 1) * P],
             )
-            nc.tensor.matmul_mx(out=ve[:], **wv4_pass, **v_pass(1), start=True, stop=False)
-            nc.tensor.matmul_mx(out=ve[:], **weight_pass(2, i), **v_pass(0), start=False, stop=True)
+            nc.tensor.matmul_mx(out=ve[:], **weight_pass(2, i), **v_pass(0), start=True, stop=False)
+            nc.tensor.matmul_mx(out=ve[:], **wv4_pass, **v_pass(1), start=False, stop=True)
             values[i] = ve
 
         def let_through(i):
@@ -188,6 +178,16 @@ def tile_list_engram_qf_silu_kernel(
 
         prepare(0)
         prepare(1)
+        wv4_plane = keep.tile([P, N // 4], I32, name="wv4_plane", tag="grouped1_0", align_bytes=64)
+        nc.vector.memset(wv4_plane[:], 0)
+        load_scale_rows(nc.scalar, wv4_plane, wv4_scales, 1)
+        load_rows(res, "res", 0, 2, res_sb, "grouped1_6")
+        load_rows(st, "st", 4, 6, st_sb)
+        load_rows(res, "res", 2, 3, res_sb)
+        load_rows(st, "st", 6, 8, st_sb)
+        load_rows(res, "res", 3, 4, res_sb)
+        load_rows(res, "res", 4, 5, res_sb)
+        load_rows(res, "res", 5, 8, res_sb)
         prepare(2)
         for i in range(0, 3):
             key(i)

@@ -76,8 +76,8 @@ def tile_list_engram_qf_silu_kernel(
         load_weight(1, 0, 8)
         load_weight(2, 0, 8)
         load_rows(st, "st", 0, 2, st_sb)
-        nc.sync.dma_start(out=wv4_codes[:].bitcast(I32), in_=wv4_words[0].bitcast(I32))
         load_rows(st, "st", 2, 4, st_sb)
+        nc.sync.dma_start(out=wv4_codes[:].bitcast(I32), in_=wv4_words[0].bitcast(I32))
 
         picked_words = keep.tile([P, J], U32, name="picked_words", align_bytes=64)
         picked_scales = keep.tile([P, 2 * J], U8, name="picked_scales", align_bytes=64)
@@ -105,14 +105,16 @@ def tile_list_engram_qf_silu_kernel(
 
         def interleave(w, a, b, engine):
             t, first = raw[(w, a)]
-            g = keep.tile([P, (b - a) * P, PACK], BF16, name="grouped%d_%d" % (w, a), align_bytes=64)
-            dst = g[:].rearrange("p (c i) t -> p c t i", i=4)
+            pair = a - a % 2
+            if (w, pair) not in grouped:
+                grouped[(w, pair)] = keep.tile([P, 2 * P, PACK], BF16, name="grouped%d_%d" % (w, pair), align_bytes=64)
+            g = grouped[(w, pair)]
+            dst = g[:, (a - pair) * P:(b - pair) * P, :].rearrange("p (c i) t -> p c t i", i=4)
             src = t[:, :, (a - first) * P:(b - first) * P].rearrange("p t (c i) -> p c t i", i=4)
             if engine == "V":
                 nc.vector.tensor_copy(out=dst, in_=src)
             else:
                 nc.scalar.copy(out=dst, in_=src)
-            grouped[(w, a)] = g
 
         def quantize(w, a, b):
             cols = slice(a * P, b * P)
@@ -137,6 +139,12 @@ def tile_list_engram_qf_silu_kernel(
             nc.tensor.matmul_mx(out=ke[:], **weight_pass(0, i), **v_pass(0), start=True, stop=False)
             nc.tensor.matmul_mx(out=ke[:], **weight_pass(1, i), **v_pass(1), start=False, stop=True)
             keys[i] = ke
+            if i < 3:
+                keys[i] = keep.tile([P, J], F32, name="ke_copy%d" % i)
+                if i < 2:
+                    nc.vector.tensor_copy(out=keys[i][:], in_=ke[:])
+                else:
+                    nc.scalar.copy(out=keys[i][:], in_=ke[:])
 
         def gate(i):
             f = ring.tile([P, J], F32, name="f")
@@ -156,14 +164,17 @@ def tile_list_engram_qf_silu_kernel(
             values[i] = ve
 
         def let_through(i):
-            gv = keep.tile([P, J], F32, name="gated%d" % i)
-            nc.vector.tensor_tensor(out=gv[:], in0=values[i][:], in1=gates[i][:], op=MULT)
+            if i % 2 == 1 and i + 1 < TILES:
+                gv = st_sb[i + 1]
+            else:
+                gv = keep.tile([P, J], F32, name="gated%d" % i)[:]
+            nc.vector.tensor_tensor(out=gv, in0=values[i][:], in1=gates[i][:], op=MULT)
             gated[i] = gv
 
         def finish(a, b, engine, tag, group, align):
             t = keep.tile([P, b - a, J], F32, name="result%d" % a, tag=tag, align_bytes=align)
             for i in range(a, b):
-                engine.tensor_tensor(out=t[:, i - a, :], in0=gated[i][:], in1=res_sb[i], op=ADD)
+                engine.tensor_tensor(out=t[:, i - a, :], in0=gated[i], in1=res_sb[i], op=ADD)
                 if (i - a + 1) % group == 0:
                     s = i + 1 - group
                     rows = out[s * P:(i + 1) * P, :].rearrange("(t p) j -> p t j", p=P)
@@ -181,17 +192,28 @@ def tile_list_engram_qf_silu_kernel(
         wv4_plane = keep.tile([P, N // 4], I32, name="wv4_plane", tag="grouped1_0", align_bytes=64)
         nc.vector.memset(wv4_plane[:], 0)
         load_scale_rows(nc.scalar, wv4_plane, wv4_scales, 1)
-        load_rows(res, "res", 0, 2, res_sb, "grouped1_6")
+        load_rows(res, "res", 0, 1, res_sb, "grouped1_6")
         load_rows(st, "st", 4, 6, st_sb)
+        load_rows(res, "res", 1, 2, res_sb)
         load_rows(res, "res", 2, 3, res_sb)
         load_rows(st, "st", 6, 8, st_sb)
         load_rows(res, "res", 3, 4, res_sb)
         load_rows(res, "res", 4, 5, res_sb)
         load_rows(res, "res", 5, 8, res_sb)
-        prepare(2)
-        for i in range(0, 3):
-            key(i)
+        key(0)
+        key(1)
+        key(2)
+        interleave(2, 0, 2, "V")
+        interleave(2, 2, 4, "S")
+        interleave(2, 4, 5, "V")
+        interleave(2, 5, 6, "S")
+        interleave(2, 6, 8, "S")
+        quantize(2, 0, 2)
+        for i in range(2):
+            quantize(2, 2 * i + 2, 2 * i + 4)
             gate(i)
+        gate(2)
+        quantize(2, 6, 8)
         for i in range(TILES):
             value(i)
             let_through(i)

@@ -50,8 +50,8 @@ def tile_list_engram_qf_silu_kernel(
         st_sb = {}
         res_sb = {}
 
-        def load_weight(w, a, b):
-            t = keep.tile([P, PACK, (b - a) * P], F32, name="raw%d_%d" % (w, a))
+        def load_weight(w, a, b, tag=None):
+            t = keep.tile([P, PACK, (b - a) * P], F32, name="raw%d_%d" % (w, a), tag=tag or "raw%d" % w, align_bytes=64)
             nc.sync.dma_start(out=t[:], in_=sources[w][:, a * P:b * P].rearrange("(p j) c -> p j c", j=PACK))
             for i in range(a, b):
                 raw[(w, i)] = (t, a)
@@ -71,13 +71,12 @@ def tile_list_engram_qf_silu_kernel(
 
         nc.sync.dma_start(out=table_words[:], in_=tab_words[0].rearrange("p t b -> p (t b)").bitcast(I32))
         nc.sync.dma_start(offsets[:], offs)
-        load_scale_rows(nc.sync, table_scales, tab_scales, 2)
+        nc.sync.dma_start(
+            out=table_scales[0:P:8, :].rearrange("q (a t) -> q a t", a=2),
+            in_=tab_scales.bitcast(I32).rearrange("a q t -> q a t"),
+        )
         load_weight(0, 0, 8)
         load_weight(1, 0, 8)
-        load_weight(2, 0, 8)
-        load_rows(st, "st", 0, 2, st_sb)
-        load_rows(st, "st", 2, 4, st_sb)
-        nc.sync.dma_start(out=wv4_codes[:].bitcast(I32), in_=wv4_words[0].bitcast(I32))
 
         picked_words = keep.tile([P, J], U32, name="picked_words", align_bytes=64)
         picked_scales = keep.tile([P, 2 * J], U8, name="picked_scales", align_bytes=64)
@@ -93,10 +92,15 @@ def tile_list_engram_qf_silu_kernel(
                 in_=table_scales[:].bitcast(U8)[:, a * T:(a + 1) * T].indirect(offsets[:]),
             )
 
+        v_planes = keep.tile([P, 2 * J // 4], I32, name="v_planes", align_bytes=64)
+        nc.vector.tensor_copy(out=v_planes[:], in_=picked_scales[:].bitcast(I32))
+        for r in range(1, 4):
+            nc.scalar.dma_start(out=v_planes[r:P:32, :], in_=v_planes[8 * r:P:32, :])
+
         def v_pass(a):
             return dict(
                 rhs=v_codes[:, 2 * J * a:2 * J * (a + 1)].bitcast(FP4X4),
-                rhs_scale=picked_scales[:, a * J:(a + 1) * J],
+                rhs_scale=v_planes[:].bitcast(U8)[:, a * J:(a + 1) * J],
             )
 
         codes = [keep.tile([P, N], U32, name="codes%d" % w, align_bytes=64) for w in range(3)]
@@ -188,6 +192,10 @@ def tile_list_engram_qf_silu_kernel(
                 quantize(w, c, c + 2)
 
         prepare(0)
+        load_weight(2, 0, 8, "grouped0_0")
+        load_rows(st, "st", 0, 2, st_sb)
+        load_rows(st, "st", 2, 4, st_sb)
+        nc.sync.dma_start(out=wv4_codes[:].bitcast(I32), in_=wv4_words[0].bitcast(I32))
         prepare(1)
         wv4_plane = keep.tile([P, N // 4], I32, name="wv4_plane", tag="grouped1_0", align_bytes=64)
         nc.vector.memset(wv4_plane[:], 0)

@@ -20,9 +20,11 @@ SILU = mybir.ActivationFunctionType.Silu
 P = 128
 PACK = 4
 K_PASS = P * PACK
-HALF = 512
-PIECE = 256
 TILES = N // P
+PAIRS = TILES // 2
+POOL_SUMS = 5
+KEY_BANKS = 5
+VALUE_BANKS = 3
 
 
 def tile_list_engram_qf_silu_kernel(
@@ -31,8 +33,7 @@ def tile_list_engram_qf_silu_kernel(
     nc = tc.nc
     with ExitStack() as ctx:
         keep = ctx.enter_context(tc.tile_pool(name="keep", bufs=1))
-        ring = ctx.enter_context(tc.tile_pool(name="ring", bufs=4))
-        psum = ctx.enter_context(tc.psum_pool(name="psum", bufs=4))
+        psum = ctx.enter_context(tc.psum_pool(name="psum", bufs=1))
 
         offsets = keep.tile([P, J // 16], U16, name="offsets")
         table_words = keep.tile([P, T], I32, name="table_words", align_bytes=64)
@@ -41,7 +42,11 @@ def tile_list_engram_qf_silu_kernel(
         warm_in = keep.tile([P, 8], F32, name="warm_in")
         warm_out = keep.tile([P, 8], F32, name="warm_out")
 
+        given_planes = keep.tile([P, (2 * J + N) // 4], I32, name="given_planes", align_bytes=64)
+        v_planes = given_planes[:, 0:2 * J // 4]
+        wv4_plane = given_planes[:, 2 * J // 4:]
         nc.vector.memset(table_scales[:], 0)
+        nc.vector.memset(wv4_plane, 0)
         nc.vector.memset(warm_in[:], 0.0)
         nc.scalar.activation(out=warm_out[:], in_=warm_in[:], func=SILU)
 
@@ -50,24 +55,16 @@ def tile_list_engram_qf_silu_kernel(
         st_sb = {}
         res_sb = {}
 
-        def load_weight(w, a, b, tag=None):
-            t = keep.tile([P, PACK, (b - a) * P], F32, name="raw%d_%d" % (w, a), tag=tag or "raw%d" % w, align_bytes=64)
-            nc.sync.dma_start(out=t[:], in_=sources[w][:, a * P:b * P].rearrange("(p j) c -> p j c", j=PACK))
-            for i in range(a, b):
-                raw[(w, i)] = (t, a)
+        def load_weight(w, t0, t1, tag):
+            raw[(w, t0)] = keep.tile([P, t1 - t0, N], F32, name="raw%d_%d" % (w, t0), tag=tag, align_bytes=64)
+            rows = sources[w].rearrange("(p t) c -> p t c", t=PACK)
+            nc.sync.dma_start(out=raw[(w, t0)][:], in_=rows[:, t0:t1, :])
 
-        def load_rows(src, name, a, b, into, tag=None):
-            t = keep.tile([P, b - a, J], F32, name="%s%d" % (name, a), tag=tag or "%s%d" % (name, a), align_bytes=64)
-            nc.sync.dma_start(out=t[:], in_=src[a * P:b * P, :].rearrange("(t p) j -> p t j", p=P))
+        def load_tiles(src, name, a, b, into):
+            t = keep.tile([P, b - a, J], F32, name="%s%d" % (name, a), align_bytes=64)
+            nc.sync.dma_start(out=t[:], in_=src[a * P:b * P, :].rearrange("(i p) j -> p i j", p=P))
             for i in range(a, b):
                 into[i] = t[:, i - a, :]
-
-        def load_scale_rows(queue, plane, rows, passes):
-            for r in range(4):
-                queue.dma_start(
-                    out=plane[r:P:32, :].rearrange("q (a t) -> q a t", a=passes),
-                    in_=rows[:, r:16:4, :].bitcast(I32).rearrange("a q t -> q a t"),
-                )
 
         nc.sync.dma_start(out=table_words[:], in_=tab_words[0].rearrange("p t b -> p (t b)").bitcast(I32))
         nc.sync.dma_start(offsets[:], offs)
@@ -75,158 +72,135 @@ def tile_list_engram_qf_silu_kernel(
             out=table_scales[0:P:8, :].rearrange("q (a t) -> q a t", a=2),
             in_=tab_scales.bitcast(I32).rearrange("a q t -> q a t"),
         )
-        load_weight(0, 0, 8)
-        load_weight(1, 0, 8)
+        nc.sync.dma_start(out=given_planes[0:P:8, 2 * J // 4:], in_=wv4_scales[0].bitcast(I32))
+        load_weight(0, 0, PACK, "raw0")
+        load_weight(1, 0, PACK, "raw1")
 
-        picked_words = keep.tile([P, J], U32, name="picked_words", align_bytes=64)
-        picked_scales = keep.tile([P, 2 * J], U8, name="picked_scales", align_bytes=64)
+        picked_scales = keep.tile([P, 2 * J], U8, name="picked_scales", tag="picked", align_bytes=64)
         v_codes = keep.tile([P, 2 * 2 * J], U8, name="v_codes", align_bytes=64)
-        nc.vector.tensor_copy(out=picked_words[:], in_=table_words[:].bitcast(U32).indirect(offsets[:]))
-        nc.vector.tensor_copy(
-            out=v_codes[:].bitcast(U16).rearrange("p (d j) -> p d j", d=2),
-            in_=picked_words[:].bitcast(U16).rearrange("p (j d) -> p d j", d=2),
-        )
         for a in range(2):
             nc.vector.tensor_copy(
                 out=picked_scales[:, a * J:(a + 1) * J],
                 in_=table_scales[:].bitcast(U8)[:, a * T:(a + 1) * T].indirect(offsets[:]),
             )
-
-        v_planes = keep.tile([P, 2 * J // 4], I32, name="v_planes", align_bytes=64)
-        nc.vector.tensor_copy(out=v_planes[:], in_=picked_scales[:].bitcast(I32))
+        nc.vector.tensor_copy(out=v_planes, in_=picked_scales[:].bitcast(I32))
         for r in range(1, 4):
-            nc.scalar.dma_start(out=v_planes[r:P:32, :], in_=v_planes[8 * r:P:32, :])
+            nc.scalar.dma_start(out=given_planes[r:P:32, :], in_=given_planes[8 * r:P:32, :])
+        picked_words = keep.tile([P, J], U32, name="picked_words", tag="picked", align_bytes=64)
+        nc.vector.tensor_copy(out=picked_words[:], in_=table_words[:].bitcast(U32).indirect(offsets[:]))
+        nc.vector.tensor_copy(
+            out=v_codes[:].bitcast(U16).rearrange("p (d j) -> p d j", d=2),
+            in_=picked_words[:].bitcast(U16).rearrange("p (j d) -> p d j", d=2),
+        )
 
         def v_pass(a):
             return dict(
                 rhs=v_codes[:, 2 * J * a:2 * J * (a + 1)].bitcast(FP4X4),
-                rhs_scale=v_planes[:].bitcast(U8)[:, a * J:(a + 1) * J],
+                rhs_scale=v_planes.bitcast(U8)[:, a * J:(a + 1) * J],
             )
 
         codes = [keep.tile([P, N], U32, name="codes%d" % w, align_bytes=64) for w in range(3)]
         planes = [keep.tile([P, N], U8, name="planes%d" % w, align_bytes=64) for w in range(3)]
         grouped = {}
 
-        def interleave(w, a, b, engine):
-            t, first = raw[(w, a)]
-            pair = a - a % 2
+        def interleave(w, a, b, t0, t1, copy):
+            pair = a // 2
             if (w, pair) not in grouped:
                 grouped[(w, pair)] = keep.tile([P, 2 * P, PACK], BF16, name="grouped%d_%d" % (w, pair), align_bytes=64)
-            g = grouped[(w, pair)]
-            dst = g[:, (a - pair) * P:(b - pair) * P, :].rearrange("p (c i) t -> p c t i", i=4)
-            src = t[:, :, (a - first) * P:(b - first) * P].rearrange("p t (c i) -> p c t i", i=4)
-            if engine == "V":
-                nc.vector.tensor_copy(out=dst, in_=src)
-            else:
-                nc.scalar.copy(out=dst, in_=src)
+            dst = grouped[(w, pair)][:, (a - 2 * pair) * P:(b - 2 * pair) * P, t0:t1]
+            src = raw[(w, t0)][:, :, a * P:b * P]
+            copy(out=dst.rearrange("p (c i) t -> p c t i", i=4), in_=src.rearrange("p t (c i) -> p c t i", i=4))
 
-        def quantize(w, a, b):
-            cols = slice(a * P, b * P)
+        def quantize(w, pair):
+            cols = slice(2 * pair * P, 2 * (pair + 1) * P)
             nc.vector.quantize_mx(
                 out=codes[w][:, cols].bitcast(FP8X4),
                 scales=planes[w][:, cols],
-                in_=grouped[(w, a)][:].rearrange("p c t -> p (c t)"),
+                in_=grouped[(w, pair)][:].rearrange("p c t -> p (c t)"),
             )
 
         def weight_pass(w, i):
             cols = slice(i * P, (i + 1) * P)
             return dict(lhsT=codes[w][:, cols].bitcast(FP8X4), lhsT_scale=planes[w][:, cols])
 
-        gates = {}
-        gated = {}
+        on_vector, on_scalar = nc.vector.tensor_copy, nc.scalar.copy
+
+        def prepare(w):
+            for pair in range(PAIRS):
+                interleave(w, 2 * pair, 2 * pair + 2, 0, PACK, on_vector if pair % 2 == 0 else on_scalar)
+            for pair in range(PAIRS):
+                quantize(w, pair)
 
         keys = {}
         values = {}
+        gates = {}
+        gated = {}
 
         def key(i):
-            ke = psum.tile([P, J], F32, name="ke", bufs=5)
-            nc.tensor.matmul_mx(out=ke[:], **weight_pass(0, i), **v_pass(0), start=True, stop=False)
-            nc.tensor.matmul_mx(out=ke[:], **weight_pass(1, i), **v_pass(1), start=False, stop=True)
-            keys[i] = ke
-            if i < 3:
-                keys[i] = keep.tile([P, J], F32, name="ke_copy%d" % i)
-                if i < 2:
-                    nc.vector.tensor_copy(out=keys[i][:], in_=ke[:])
-                else:
-                    nc.scalar.copy(out=keys[i][:], in_=ke[:])
+            keys[i] = psum.tile([P, J], F32, name="key%d" % i, tag="key", bufs=KEY_BANKS)
+            nc.tensor.matmul_mx(out=keys[i][:], **weight_pass(0, i), **v_pass(0), start=True, stop=False)
+            nc.tensor.matmul_mx(out=keys[i][:], **weight_pass(1, i), **v_pass(1), start=False, stop=True)
 
         def gate(i):
-            f = ring.tile([P, J], F32, name="f")
+            f = keep.tile([P, J], F32, name="f%d" % i, align_bytes=64)
             nc.vector.tensor_tensor(out=f[:], in0=keys[i][:], in1=st_sb[i], op=MULT)
-            g = keep.tile([P, J], F32, name="gate%d" % i, tag="late" if i == TILES - 2 else "gate%d" % i)
-            nc.scalar.activation(out=g[:], in_=f[:], func=SILU)
-            gates[i] = g
+            gates[i] = keep.tile([P, J], F32, name="gate%d" % i, tag="late" if i == TILES - 2 else "gate%d" % i, align_bytes=64)
+            nc.scalar.activation(out=gates[i][:], in_=f[:], func=SILU)
 
         def value(i):
-            ve = psum.tile([P, J], F32, name="ve", bufs=3)
+            values[i] = psum.tile([P, J], F32, name="value%d" % i, tag="value", bufs=VALUE_BANKS)
             wv4_pass = dict(
                 lhsT=wv4_codes[:, 2 * P * i:2 * P * (i + 1)].bitcast(FP4X4),
-                lhsT_scale=wv4_plane[:].bitcast(U8)[:, i * P:(i + 1) * P],
+                lhsT_scale=wv4_plane.bitcast(U8)[:, i * P:(i + 1) * P],
             )
-            nc.tensor.matmul_mx(out=ve[:], **weight_pass(2, i), **v_pass(0), start=True, stop=False)
-            nc.tensor.matmul_mx(out=ve[:], **wv4_pass, **v_pass(1), start=False, stop=True)
-            values[i] = ve
+            nc.tensor.matmul_mx(out=values[i][:], **weight_pass(2, i), **v_pass(0), start=True, stop=False)
+            nc.tensor.matmul_mx(out=values[i][:], **wv4_pass, **v_pass(1), start=False, stop=True)
 
         def let_through(i):
-            if i % 2 == 1 and i + 1 < TILES:
-                gv = st_sb[i + 1]
-            else:
-                gv = keep.tile([P, J], F32, name="gated%d" % i)[:]
-            nc.vector.tensor_tensor(out=gv, in0=values[i][:], in1=gates[i][:], op=MULT)
-            gated[i] = gv
+            gated[i] = keep.tile([P, J], F32, name="gated%d" % i)[:]
+            nc.vector.tensor_tensor(out=gated[i], in0=values[i][:], in1=gates[i][:], op=MULT)
 
-        def finish(a, b, engine, tag, group, align):
-            t = keep.tile([P, b - a, J], F32, name="result%d" % a, tag=tag, align_bytes=align)
+        def finish(a, b, engine, tag):
+            t = keep.tile([P, b - a, J], F32, name="result%d" % a, tag=tag, align_bytes=64)
             for i in range(a, b):
                 engine.tensor_tensor(out=t[:, i - a, :], in0=gated[i], in1=res_sb[i], op=ADD)
-                if (i - a + 1) % group == 0:
-                    s = i + 1 - group
-                    rows = out[s * P:(i + 1) * P, :].rearrange("(t p) j -> p t j", p=P)
-                    nc.sync.dma_start(out=rows, in_=t[:, s - a:i + 1 - a, :])
+                nc.sync.dma_start(out=out[i * P:(i + 1) * P, :], in_=t[:, i - a, :])
 
-        def prepare(w):
-            for c in range(0, TILES, 4):
-                interleave(w, c, c + 2, "V")
-                interleave(w, c + 2, c + 4, "S")
-            for c in range(0, TILES, 2):
-                quantize(w, c, c + 2)
-
-        prepare(0)
-        load_weight(2, 0, 8, "grouped0_0")
-        load_rows(st, "st", 0, 2, st_sb)
-        load_rows(st, "st", 2, 4, st_sb)
+        load_weight(2, 0, 2, "table_words")
+        load_weight(2, 2, PACK, "raw2")
+        load_tiles(st, "st", 0, 2, st_sb)
         nc.sync.dma_start(out=wv4_codes[:].bitcast(I32), in_=wv4_words[0].bitcast(I32))
+        load_tiles(st, "st", 2, 4, st_sb)
+        load_tiles(res, "res", 0, 1, res_sb)
+        for i in range(1, POOL_SUMS):
+            load_tiles(st, "st", i + 3, i + 4, st_sb)
+            load_tiles(res, "res", i, i + 1, res_sb)
+        load_tiles(res, "res", POOL_SUMS, TILES, res_sb)
+        prepare(0)
         prepare(1)
-        wv4_plane = keep.tile([P, N // 4], I32, name="wv4_plane", tag="grouped1_0", align_bytes=64)
-        nc.vector.memset(wv4_plane[:], 0)
-        load_scale_rows(nc.scalar, wv4_plane, wv4_scales, 1)
-        load_rows(res, "res", 0, 1, res_sb, "grouped1_6")
-        load_rows(st, "st", 4, 6, st_sb)
-        load_rows(res, "res", 1, 2, res_sb)
-        load_rows(res, "res", 2, 3, res_sb)
-        load_rows(st, "st", 6, 8, st_sb)
-        load_rows(res, "res", 3, 4, res_sb)
-        load_rows(res, "res", 4, 5, res_sb)
-        load_rows(res, "res", 5, 8, res_sb)
-        key(0)
-        key(1)
-        key(2)
-        interleave(2, 0, 2, "V")
-        interleave(2, 2, 4, "S")
-        interleave(2, 4, 5, "V")
-        interleave(2, 5, 6, "S")
-        interleave(2, 6, 8, "S")
-        quantize(2, 0, 2)
-        for i in range(2):
-            quantize(2, 2 * i + 2, 2 * i + 4)
-            gate(i)
-        gate(2)
-        quantize(2, 6, 8)
+        for i in range(KEY_BANKS):
+            key(i)
+        for pair in range(PAIRS):
+            interleave(2, 2 * pair, 2 * pair + 2, 0, 2, on_vector if pair < 3 else on_scalar)
+        interleave(2, 0, 2, 2, PACK, on_vector)
+        interleave(2, 2, 4, 2, PACK, on_scalar)
+        interleave(2, 4, 5, 2, PACK, on_vector)
+        interleave(2, 5, 6, 2, PACK, on_scalar)
+        interleave(2, 6, 8, 2, PACK, on_scalar)
+        quantize(2, 0)
+        quantize(2, 1)
+        gate(0)
+        quantize(2, 2)
+        gate(1)
+        quantize(2, 3)
         for i in range(TILES):
             value(i)
+            if KEY_BANKS <= i + 4 < TILES:
+                key(i + 4)
             let_through(i)
-            if i + 3 < TILES:
-                key(i + 3)
+            if i < 2:
+                gate(i + 2)
+            if 1 <= i < TILES - 3:
                 gate(i + 3)
-        finish(0, 5, nc.gpsimd, "grouped2_6", 1, 64)
-        finish(5, 8, nc.vector, "late", 1, 32)
+        finish(0, POOL_SUMS, nc.gpsimd, "grouped2_3")
+        finish(POOL_SUMS, TILES, nc.vector, "late")

@@ -24,7 +24,8 @@ TILES = N // P
 PAIRS = TILES // 2
 POOL_SUMS = 5
 KEY_BANKS = 5
-VALUE_BANKS = 3
+KEY_BANK = [0, 1, 2, 3, 4, 1, 2, 3]
+VALUE_BANK = [5, 6, 7, 0, 4, 5, 6, 7]
 
 
 def tile_list_engram_qf_silu_kernel(
@@ -137,7 +138,7 @@ def tile_list_engram_qf_silu_kernel(
         gated = {}
 
         def key(i):
-            keys[i] = psum.tile([P, J], F32, name="key%d" % i, tag="key", bufs=KEY_BANKS)
+            keys[i] = psum.tile([P, J], F32, name="key%d" % i, tag="bank%d" % KEY_BANK[i])
             nc.tensor.matmul_mx(out=keys[i][:], **weight_pass(0, i), **v_pass(0), start=True, stop=False)
             nc.tensor.matmul_mx(out=keys[i][:], **weight_pass(1, i), **v_pass(1), start=False, stop=True)
 
@@ -148,7 +149,7 @@ def tile_list_engram_qf_silu_kernel(
             nc.scalar.activation(out=gates[i][:], in_=f[:], func=SILU)
 
         def value(i):
-            values[i] = psum.tile([P, J], F32, name="value%d" % i, tag="value", bufs=VALUE_BANKS)
+            values[i] = psum.tile([P, J], F32, name="value%d" % i, tag="bank%d" % VALUE_BANK[i])
             wv4_pass = dict(
                 lhsT=wv4_codes[:, 2 * P * i:2 * P * (i + 1)].bitcast(FP4X4),
                 lhsT_scale=wv4_plane.bitcast(U8)[:, i * P:(i + 1) * P],
@@ -182,17 +183,14 @@ def tile_list_engram_qf_silu_kernel(
             key(i)
         for pair in range(PAIRS):
             interleave(2, 2 * pair, 2 * pair + 2, 0, 2, on_vector if pair < 3 else on_scalar)
-        interleave(2, 0, 2, 2, PACK, on_vector)
-        interleave(2, 2, 4, 2, PACK, on_scalar)
-        interleave(2, 4, 5, 2, PACK, on_vector)
-        interleave(2, 5, 6, 2, PACK, on_scalar)
-        interleave(2, 6, 8, 2, PACK, on_scalar)
+        for pair in range(PAIRS):
+            interleave(2, 2 * pair, 2 * pair + 2, 2, PACK, on_vector if pair % 2 == 0 else on_scalar)
         quantize(2, 0)
         quantize(2, 1)
         gate(0)
         quantize(2, 2)
-        gate(1)
         quantize(2, 3)
+        gate(1)
         for i in range(TILES):
             value(i)
             if KEY_BANKS <= i + 4 < TILES:

@@ -23,6 +23,7 @@ K_PASS = P * PACK
 TILES = N // P
 PAIRS = TILES // 2
 POOL_SUMS = 5
+SPLIT = 704
 KEY_BANKS = 5
 KEY_BANK = [0, 1, 2, 3, 4, 1, 2, 3]
 VALUE_BANK = [5, 6, 7, 0, 4, 5, 6, 7]
@@ -105,11 +106,11 @@ def tile_list_engram_qf_silu_kernel(
         grouped = {}
 
         def interleave(w, a, b, t0, t1, copy):
-            pair = a // 2
+            pair = a // (2 * P)
             if (w, pair) not in grouped:
                 grouped[(w, pair)] = keep.tile([P, 2 * P, PACK], BF16, name="grouped%d_%d" % (w, pair), align_bytes=64)
-            dst = grouped[(w, pair)][:, (a - 2 * pair) * P:(b - 2 * pair) * P, t0:t1]
-            src = raw[(w, t0)][:, :, a * P:b * P]
+            dst = grouped[(w, pair)][:, a - 2 * pair * P:b - 2 * pair * P, t0:t1]
+            src = raw[(w, t0)][:, :, a:b]
             copy(out=dst.rearrange("p (c i) t -> p c t i", i=4), in_=src.rearrange("p t (c i) -> p c t i", i=4))
 
         def quantize(w, pair):
@@ -128,7 +129,7 @@ def tile_list_engram_qf_silu_kernel(
 
         def prepare(w):
             for pair in range(PAIRS):
-                interleave(w, 2 * pair, 2 * pair + 2, 0, PACK, on_vector if pair % 2 == 0 else on_scalar)
+                interleave(w, 2 * pair * P, 2 * (pair + 1) * P, 0, PACK, on_vector if pair % 2 == 0 else on_scalar)
             for pair in range(PAIRS):
                 quantize(w, pair)
 
@@ -169,36 +170,44 @@ def tile_list_engram_qf_silu_kernel(
 
         load_weight(2, 0, 2, "table_words")
         load_weight(2, 2, PACK, "raw2")
-        load_tiles(st, "st", 0, 2, st_sb)
+        load_tiles(st, "st", 0, 1, st_sb)
+        load_tiles(st, "st", 1, 2, st_sb)
         nc.sync.dma_start(out=wv4_codes[:].bitcast(I32), in_=wv4_words[0].bitcast(I32))
         load_tiles(st, "st", 2, 4, st_sb)
         load_tiles(res, "res", 0, 1, res_sb)
-        for i in range(1, POOL_SUMS):
-            load_tiles(st, "st", i + 3, i + 4, st_sb)
-            load_tiles(res, "res", i, i + 1, res_sb)
+        load_tiles(st, "st", 4, 6, st_sb)
+        load_tiles(res, "res", 1, 2, res_sb)
+        load_tiles(st, "st", 6, 7, st_sb)
+        load_tiles(res, "res", 2, 3, res_sb)
+        load_tiles(st, "st", 7, 8, st_sb)
+        load_tiles(res, "res", 3, 4, res_sb)
+        load_tiles(res, "res", 4, 5, res_sb)
         load_tiles(res, "res", POOL_SUMS, TILES, res_sb)
         prepare(0)
         prepare(1)
         for i in range(KEY_BANKS):
             key(i)
         for pair in range(PAIRS):
-            interleave(2, 2 * pair, 2 * pair + 2, 0, 2, on_vector if pair < 3 else on_scalar)
-        for pair in range(PAIRS):
-            interleave(2, 2 * pair, 2 * pair + 2, 2, PACK, on_vector if pair % 2 == 0 else on_scalar)
+            interleave(2, 2 * pair * P, 2 * (pair + 1) * P, 0, 2, on_vector if pair < 3 else on_scalar)
+        interleave(2, 0, 256, 2, PACK, on_vector)
+        interleave(2, 256, 512, 2, PACK, on_scalar)
+        interleave(2, 512, SPLIT, 2, PACK, on_vector)
+        interleave(2, SPLIT, 768, 2, PACK, on_scalar)
+        interleave(2, 768, N, 2, PACK, on_scalar)
         quantize(2, 0)
-        quantize(2, 1)
-        gate(0)
         quantize(2, 2)
-        quantize(2, 3)
+        gate(0)
+        quantize(2, 1)
         gate(1)
+        quantize(2, 3)
         for i in range(TILES):
             value(i)
             if KEY_BANKS <= i + 4 < TILES:
                 key(i + 4)
             let_through(i)
-            if i < 2:
-                gate(i + 2)
-            if 1 <= i < TILES - 3:
+            if i == 0:
+                gate(2)
+            if i + 3 < TILES:
                 gate(i + 3)
         finish(0, POOL_SUMS, nc.gpsimd, "grouped2_3")
         finish(POOL_SUMS, TILES, nc.vector, "late")

@@ -20,6 +20,8 @@ SILU = mybir.ActivationFunctionType.Silu
 P = 128
 PACK = 4
 K_PASS = P * PACK
+DEAL = 2
+PLAIN_PAIRS = 1
 TILES = N // P
 PAIRS = TILES // 2
 POOL_SUMS = 5
@@ -40,7 +42,8 @@ def tile_list_engram_qf_silu_kernel(
         offsets = keep.tile([P, J // 16], U16, name="offsets")
         table_words = keep.tile([P, T], I32, name="table_words", align_bytes=64)
         table_scales = keep.tile([P, 2 * T // 4], I32, name="table_scales", align_bytes=64)
-        wv4_codes = keep.tile([P, 2 * N], U8, name="wv4_codes", align_bytes=64)
+        wv4_rows = keep.tile([P, N // 4], I32, name="wv4_rows", align_bytes=64)
+        wv4_raw = keep.tile([P, N // 2], I32, name="wv4_raw", align_bytes=64)
         warm_in = keep.tile([P, 8], F32, name="warm_in")
         warm_out = keep.tile([P, 8], F32, name="warm_out")
 
@@ -48,7 +51,7 @@ def tile_list_engram_qf_silu_kernel(
         v_planes = given_planes[:, 0:2 * J // 4]
         wv4_plane = given_planes[:, 2 * J // 4:]
         nc.vector.memset(table_scales[:], 0)
-        nc.vector.memset(wv4_plane, 0)
+        nc.vector.memset(wv4_rows[:], 0)
         nc.vector.memset(warm_in[:], 0.0)
         nc.scalar.activation(out=warm_out[:], in_=warm_in[:], func=SILU)
 
@@ -62,9 +65,14 @@ def tile_list_engram_qf_silu_kernel(
             rows = sources[w].rearrange("(p t) c -> p t c", t=PACK)
             nc.sync.dma_start(out=raw[(w, t0)][:], in_=rows[:, t0:t1, :])
 
+        def dealt(rows, a, b):
+            order = "(i p) j -> p i j" if a // 2 < PLAIN_PAIRS else "(p i) j -> p i j"
+            pair = rows[a // 2 * P * DEAL:(a // 2 + 1) * P * DEAL, :].rearrange(order, i=DEAL)
+            return pair[:, a % 2:a % 2 + b - a, :]
+
         def load_tiles(src, name, a, b, into):
             t = keep.tile([P, b - a, J], F32, name="%s%d" % (name, a), align_bytes=64)
-            nc.sync.dma_start(out=t[:], in_=src[a * P:b * P, :].rearrange("(i p) j -> p i j", p=P))
+            nc.sync.dma_start(out=t[:], in_=dealt(src, a, b))
             for i in range(a, b):
                 into[i] = t[:, i - a, :]
 
@@ -74,7 +82,7 @@ def tile_list_engram_qf_silu_kernel(
             out=table_scales[0:P:8, :].rearrange("q (a t) -> q a t", a=2),
             in_=tab_scales.bitcast(I32).rearrange("a q t -> q a t"),
         )
-        nc.sync.dma_start(out=given_planes[0:P:8, 2 * J // 4:], in_=wv4_scales[0].bitcast(I32))
+        nc.sync.dma_start(out=wv4_rows[0:P:8, :], in_=wv4_scales[0].bitcast(I32))
         load_weight(0, 0, PACK, "raw0")
         load_weight(1, 0, PACK, "raw1")
 
@@ -85,6 +93,12 @@ def tile_list_engram_qf_silu_kernel(
                 out=picked_scales[:, a * J:(a + 1) * J],
                 in_=table_scales[:].bitcast(U8)[:, a * T:(a + 1) * T].indirect(offsets[:]),
             )
+        plain = PLAIN_PAIRS * DEAL * P
+        nc.vector.tensor_copy(out=wv4_plane[:, 0:plain // 4], in_=wv4_rows[:, 0:plain // 4])
+        nc.vector.tensor_copy(
+            out=wv4_plane.bitcast(U8)[:, plain:].rearrange("p (h i m) -> p h i m", i=DEAL, m=P),
+            in_=wv4_rows[:].bitcast(U8)[:, plain:].rearrange("p (h m i) -> p h i m", i=DEAL, m=P),
+        )
         nc.vector.tensor_copy(out=v_planes, in_=picked_scales[:].bitcast(I32))
         for r in range(1, 4):
             nc.scalar.dma_start(out=given_planes[r:P:32, :], in_=given_planes[8 * r:P:32, :])
@@ -106,12 +120,21 @@ def tile_list_engram_qf_silu_kernel(
         grouped = {}
 
         def interleave(w, a, b, t0, t1, copy):
-            pair = a // (2 * P)
+            pair = a // (DEAL * P)
             if (w, pair) not in grouped:
-                grouped[(w, pair)] = keep.tile([P, 2 * P, PACK], BF16, name="grouped%d_%d" % (w, pair), align_bytes=64)
-            dst = grouped[(w, pair)][:, a - 2 * pair * P:b - 2 * pair * P, t0:t1]
+                grouped[(w, pair)] = keep.tile([P, DEAL * P, PACK], BF16, name="grouped%d_%d" % (w, pair), align_bytes=64)
+            first = pair * DEAL * P
             src = raw[(w, t0)][:, :, a:b]
-            copy(out=dst.rearrange("p (c i) t -> p c t i", i=4), in_=src.rearrange("p t (c i) -> p c t i", i=4))
+            if pair < PLAIN_PAIRS:
+                dst = grouped[(w, pair)][:, a - first:b - first, t0:t1]
+                copy(out=dst.rearrange("p (c m) t -> p c t m", m=4), in_=src.rearrange("p t (c m) -> p c t m", m=4))
+            else:
+                dst = grouped[(w, pair)][:].rearrange("p (i m) t -> p i m t", i=DEAL)
+                dst = dst[:, :, (a - first) // DEAL:(b - first) // DEAL, t0:t1]
+                copy(
+                    out=dst.rearrange("p i (c m) t -> p c t m i", m=2),
+                    in_=src.rearrange("p t (c m i) -> p c t m i", m=2, i=DEAL),
+                )
 
         def quantize(w, pair):
             cols = slice(2 * pair * P, 2 * (pair + 1) * P)
@@ -133,6 +156,18 @@ def tile_list_engram_qf_silu_kernel(
             for pair in range(PAIRS):
                 quantize(w, pair)
 
+        wv4_codes = {i: wv4_raw[:].bitcast(U8)[:, 2 * P * i:2 * P * (i + 1)] for i in range(PLAIN_PAIRS * DEAL)}
+
+        def deal_wv4(a, b, tag):
+            t = keep.tile([P, (b - a) * DEAL * 2 * P], U8, name="wv4_codes%d" % a, tag=tag, align_bytes=64)
+            words = wv4_raw[:].bitcast(U16)[:, a * P * DEAL:b * P * DEAL]
+            nc.scalar.copy(
+                out=t[:].bitcast(U16).rearrange("p (h i m) -> p h i m", i=DEAL, m=P),
+                in_=words.rearrange("p (h m i) -> p h i m", i=DEAL, m=P),
+            )
+            for i in range(DEAL * a, DEAL * b):
+                wv4_codes[i] = t[:, 2 * P * (i - DEAL * a):2 * P * (i - DEAL * a + 1)]
+
         keys = {}
         values = {}
         gates = {}
@@ -152,7 +187,7 @@ def tile_list_engram_qf_silu_kernel(
         def value(i):
             values[i] = psum.tile([P, J], F32, name="value%d" % i, tag="bank%d" % VALUE_BANK[i])
             wv4_pass = dict(
-                lhsT=wv4_codes[:, 2 * P * i:2 * P * (i + 1)].bitcast(FP4X4),
+                lhsT=wv4_codes[i].bitcast(FP4X4),
                 lhsT_scale=wv4_plane.bitcast(U8)[:, i * P:(i + 1) * P],
             )
             nc.tensor.matmul_mx(out=values[i][:], **weight_pass(2, i), **v_pass(0), start=True, stop=False)
@@ -166,13 +201,16 @@ def tile_list_engram_qf_silu_kernel(
             t = keep.tile([P, b - a, J], F32, name="result%d" % a, tag=tag, align_bytes=64)
             for i in range(a, b):
                 engine.tensor_tensor(out=t[:, i - a, :], in0=gated[i], in1=res_sb[i], op=ADD)
-                nc.sync.dma_start(out=out[i * P:(i + 1) * P, :], in_=t[:, i - a, :])
+                if i == 3:
+                    nc.sync.dma_start(out=dealt(out, 2, 4), in_=t[:, 2:4, :])
+                elif i != 2:
+                    nc.sync.dma_start(out=dealt(out, i, i + 1), in_=t[:, i - a:i - a + 1, :])
 
         load_weight(2, 0, 2, "table_words")
         load_weight(2, 2, PACK, "raw2")
         load_tiles(st, "st", 0, 1, st_sb)
         load_tiles(st, "st", 1, 2, st_sb)
-        nc.sync.dma_start(out=wv4_codes[:].bitcast(I32), in_=wv4_words[0].bitcast(I32))
+        nc.sync.dma_start(out=wv4_raw[:], in_=wv4_words[0].bitcast(I32))
         load_tiles(st, "st", 2, 4, st_sb)
         load_tiles(res, "res", 0, 1, res_sb)
         load_tiles(st, "st", 4, 6, st_sb)
@@ -181,8 +219,8 @@ def tile_list_engram_qf_silu_kernel(
         load_tiles(res, "res", 2, 3, res_sb)
         load_tiles(st, "st", 7, 8, st_sb)
         load_tiles(res, "res", 3, 4, res_sb)
-        load_tiles(res, "res", 4, 5, res_sb)
-        load_tiles(res, "res", POOL_SUMS, TILES, res_sb)
+        load_tiles(res, "res", 4, 6, res_sb)
+        load_tiles(res, "res", 6, 8, res_sb)
         prepare(0)
         prepare(1)
         for i in range(KEY_BANKS):
@@ -200,6 +238,7 @@ def tile_list_engram_qf_silu_kernel(
         quantize(2, 1)
         gate(1)
         quantize(2, 3)
+        deal_wv4(PLAIN_PAIRS, PAIRS, "f1")
         for i in range(TILES):
             value(i)
             if KEY_BANKS <= i + 4 < TILES:

@@ -213,10 +213,11 @@ def tile_list_engram_qf_silu_kernel(
         nc.sync.dma_start(out=wv4_raw[:], in_=wv4_words[0].bitcast(I32))
         load_tiles(st, "st", 2, 4, st_sb)
         load_tiles(res, "res", 0, 1, res_sb)
-        load_tiles(st, "st", 4, 6, st_sb)
+        load_tiles(st, "st", 4, 5, st_sb)
         load_tiles(res, "res", 1, 2, res_sb)
-        load_tiles(st, "st", 6, 7, st_sb)
+        load_tiles(st, "st", 5, 6, st_sb)
         load_tiles(res, "res", 2, 3, res_sb)
+        load_tiles(st, "st", 6, 7, st_sb)
         load_tiles(st, "st", 7, 8, st_sb)
         load_tiles(res, "res", 3, 4, res_sb)
         load_tiles(res, "res", 4, 6, res_sb)
@@ -244,9 +245,9 @@ def tile_list_engram_qf_silu_kernel(
             if KEY_BANKS <= i + 4 < TILES:
                 key(i + 4)
             let_through(i)
-            if i == 0:
-                gate(2)
-            if i + 3 < TILES:
+            if i < 2:
+                gate(i + 2)
+            if 1 <= i < TILES - 3:
                 gate(i + 3)
         finish(0, POOL_SUMS, nc.gpsimd, "grouped2_3")
         finish(POOL_SUMS, TILES, nc.vector, "late")

from contextlib import ExitStack

import concourse.mybir as mybir

K, N, T, J = 1024, 1024, 1024, 512
FLOPS = 2 * 2 * K * N * J

F32 = mybir.dt.float32
BF16 = mybir.dt.bfloat16
I32 = mybir.dt.int32
U32 = mybir.dt.uint32
U16 = mybir.dt.uint16
U8 = mybir.dt.uint8
FP8X4 = mybir.dt.float8_e4m3fn_x4
FP4X4 = mybir.dt.float4_e2m1fn_x4
MULT = mybir.AluOpType.mult
ADD = mybir.AluOpType.add
SILU = mybir.ActivationFunctionType.Silu

P = 128
PACK = 4
K_PASS = P * PACK
DEAL = 2
PLAIN_PAIRS = 1
TILES = N // P
PAIRS = TILES // 2
POOL_SUMS = 5
SPLIT = 704
KEY_BANKS = 5
KEY_BANK = [0, 1, 2, 3, 4, 1, 2, 3]
VALUE_BANK = [5, 6, 7, 0, 4, 5, 6, 7]


def tile_list_engram_qf_silu_kernel(
    tc, tab_words, tab_scales, wk, wv8, wv4_words, wv4_scales, st, res, offs, out
):
    nc = tc.nc
    with ExitStack() as ctx:
        keep = ctx.enter_context(tc.tile_pool(name="keep", bufs=1))
        psum = ctx.enter_context(tc.psum_pool(name="psum", bufs=1))

        offsets = keep.tile([P, J // 16], U16, name="offsets")
        table_words = keep.tile([P, T], I32, name="table_words", align_bytes=64)
        table_scales = keep.tile([P, 2 * T // 4], I32, name="table_scales", align_bytes=64)
        wv4_rows = keep.tile([P, N // 4], I32, name="wv4_rows", align_bytes=64)
        wv4_raw = keep.tile([P, N // 2], I32, name="wv4_raw", align_bytes=64)
        warm_in = keep.tile([P, 8], F32, name="warm_in")
        warm_out = keep.tile([P, 8], F32, name="warm_out")

        given_planes = keep.tile([P, (2 * J + N) // 4], I32, name="given_planes", align_bytes=64)
        v_planes = given_planes[:, 0:2 * J // 4]
        wv4_plane = given_planes[:, 2 * J // 4:]
        nc.vector.memset(table_scales[:], 0)
        nc.vector.memset(wv4_rows[:], 0)
        nc.vector.memset(warm_in[:], 0.0)
        nc.scalar.activation(out=warm_out[:], in_=warm_in[:], func=SILU)

        sources = [wk[0:K_PASS, :], wk[K_PASS:K, :], wv8]
        raw = {}
        st_sb = {}
        res_sb = {}

        def load_weight(w, t0, t1, tag):
            raw[(w, t0)] = keep.tile([P, t1 - t0, N], F32, name="raw%d_%d" % (w, t0), tag=tag, align_bytes=64)
            rows = sources[w].rearrange("(p t) c -> p t c", t=PACK)
            nc.sync.dma_start(out=raw[(w, t0)][:], in_=rows[:, t0:t1, :])

        def dealt(rows, a, b):
            order = "(i p) j -> p i j" if a // 2 < PLAIN_PAIRS else "(p i) j -> p i j"
            pair = rows[a // 2 * P * DEAL:(a // 2 + 1) * P * DEAL, :].rearrange(order, i=DEAL)
            return pair[:, a % 2:a % 2 + b - a, :]

        def load_tiles(src, name, a, b, into):
            t = keep.tile([P, b - a, J], F32, name="%s%d" % (name, a), align_bytes=64)
            nc.sync.dma_start(out=t[:], in_=dealt(src, a, b))
            for i in range(a, b):
                into[i] = t[:, i - a, :]

        nc.sync.dma_start(out=table_words[:], in_=tab_words[0].rearrange("p t b -> p (t b)").bitcast(I32))
        nc.sync.dma_start(offsets[:], offs)
        nc.sync.dma_start(
            out=table_scales[0:P:8, :].rearrange("q (a t) -> q a t", a=2),
            in_=tab_scales.bitcast(I32).rearrange("a q t -> q a t"),
        )
        nc.sync.dma_start(out=wv4_rows[0:P:8, :], in_=wv4_scales[0].bitcast(I32))
        load_weight(0, 0, PACK, "raw0")
        load_weight(1, 0, PACK, "raw1")

        picked_scales = keep.tile([P, 2 * J], U8, name="picked_scales", tag="picked", align_bytes=64)
        v_codes = keep.tile([P, 2 * 2 * J], U8, name="v_codes", align_bytes=64)
        for a in range(2):
            nc.vector.tensor_copy(
                out=picked_scales[:, a * J:(a + 1) * J],
                in_=table_scales[:].bitcast(U8)[:, a * T:(a + 1) * T].indirect(offsets[:]),
            )
        plain = PLAIN_PAIRS * DEAL * P
        nc.vector.tensor_copy(out=wv4_plane[:, 0:plain // 4], in_=wv4_rows[:, 0:plain // 4])
        nc.vector.tensor_copy(
            out=wv4_plane.bitcast(U8)[:, plain:].rearrange("p (h i m) -> p h i m", i=DEAL, m=P),
            in_=wv4_rows[:].bitcast(U8)[:, plain:].rearrange("p (h m i) -> p h i m", i=DEAL, m=P),
        )
        nc.vector.tensor_copy(out=v_planes, in_=picked_scales[:].bitcast(I32))
        for r in range(1, 4):
            nc.scalar.dma_start(out=given_planes[r:P:32, :], in_=given_planes[8 * r:P:32, :])
        picked_words = keep.tile([P, J], U32, name="picked_words", tag="picked", align_bytes=64)
        nc.vector.tensor_copy(out=picked_words[:], in_=table_words[:].bitcast(U32).indirect(offsets[:]))
        nc.vector.tensor_copy(
            out=v_codes[:].bitcast(U16).rearrange("p (d j) -> p d j", d=2),
            in_=picked_words[:].bitcast(U16).rearrange("p (j d) -> p d j", d=2),
        )

        def v_pass(a):
            return dict(
                rhs=v_codes[:, 2 * J * a:2 * J * (a + 1)].bitcast(FP4X4),
                rhs_scale=v_planes.bitcast(U8)[:, a * J:(a + 1) * J],
            )

        codes = [keep.tile([P, N], U32, name="codes%d" % w, align_bytes=64) for w in range(3)]
        planes = [keep.tile([P, N], U8, name="planes%d" % w, align_bytes=64) for w in range(3)]
        grouped = {}

        def interleave(w, a, b, t0, t1, copy):
            pair = a // (DEAL * P)
            if (w, pair) not in grouped:
                grouped[(w, pair)] = keep.tile([P, DEAL * P, PACK], BF16, name="grouped%d_%d" % (w, pair), align_bytes=64)
            first = pair * DEAL * P
            src = raw[(w, t0)][:, :, a:b]
            if pair < PLAIN_PAIRS:
                dst = grouped[(w, pair)][:, a - first:b - first, t0:t1]
                copy(out=dst.rearrange("p (c m) t -> p c t m", m=4), in_=src.rearrange("p t (c m) -> p c t m", m=4))
            else:
                dst = grouped[(w, pair)][:].rearrange("p (i m) t -> p i m t", i=DEAL)
                dst = dst[:, :, (a - first) // DEAL:(b - first) // DEAL, t0:t1]
                copy(
                    out=dst.rearrange("p i (c m) t -> p c t m i", m=2),
                    in_=src.rearrange("p t (c m i) -> p c t m i", m=2, i=DEAL),
                )

        def quantize(w, pair):
            cols = slice(2 * pair * P, 2 * (pair + 1) * P)
            nc.vector.quantize_mx(
                out=codes[w][:, cols].bitcast(FP8X4),
                scales=planes[w][:, cols],
                in_=grouped[(w, pair)][:].rearrange("p c t -> p (c t)"),
            )

        def weight_pass(w, i):
            cols = slice(i * P, (i + 1) * P)
            return dict(lhsT=codes[w][:, cols].bitcast(FP8X4), lhsT_scale=planes[w][:, cols])

        on_vector, on_scalar = nc.vector.tensor_copy, nc.scalar.copy

        def prepare(w):
            for pair in range(PAIRS):
                interleave(w, 2 * pair * P, 2 * (pair + 1) * P, 0, PACK, on_vector if pair % 2 == 0 else on_scalar)
            for pair in range(PAIRS):
                quantize(w, pair)

        wv4_codes = {i: wv4_raw[:].bitcast(U8)[:, 2 * P * i:2 * P * (i + 1)] for i in range(PLAIN_PAIRS * DEAL)}

        def deal_wv4(a, b, tag):
            t = keep.tile([P, (b - a) * DEAL * 2 * P], U8, name="wv4_codes%d" % a, tag=tag, align_bytes=64)
            words = wv4_raw[:].bitcast(U16)[:, a * P * DEAL:b * P * DEAL]
            nc.scalar.copy(
                out=t[:].bitcast(U16).rearrange("p (h i m) -> p h i m", i=DEAL, m=P),
                in_=words.rearrange("p (h m i) -> p h i m", i=DEAL, m=P),
            )
            for i in range(DEAL * a, DEAL * b):
                wv4_codes[i] = t[:, 2 * P * (i - DEAL * a):2 * P * (i - DEAL * a + 1)]

        keys = {}
        values = {}
        gates = {}
        gated = {}

        def key(i):
            keys[i] = psum.tile([P, J], F32, name="key%d" % i, tag="bank%d" % KEY_BANK[i])
            nc.tensor.matmul_mx(out=keys[i][:], **weight_pass(0, i), **v_pass(0), start=True, stop=False)
            nc.tensor.matmul_mx(out=keys[i][:], **weight_pass(1, i), **v_pass(1), start=False, stop=True)

        def gate(i):
            f = keep.tile([P, J], F32, name="f%d" % i, align_bytes=64)
            nc.vector.tensor_tensor(out=f[:], in0=keys[i][:], in1=st_sb[i], op=MULT)
            gates[i] = keep.tile([P, J], F32, name="gate%d" % i, tag="late" if i == TILES - 2 else "gate%d" % i, align_bytes=64)
            nc.scalar.activation(out=gates[i][:], in_=f[:], func=SILU)

        def value(i):
            values[i] = psum.tile([P, J], F32, name="value%d" % i, tag="bank%d" % VALUE_BANK[i])
            wv4_pass = dict(
                lhsT=wv4_codes[i].bitcast(FP4X4),
                lhsT_scale=wv4_plane.bitcast(U8)[:, i * P:(i + 1) * P],
            )
            nc.tensor.matmul_mx(out=values[i][:], **weight_pass(2, i), **v_pass(0), start=True, stop=False)
            nc.tensor.matmul_mx(out=values[i][:], **wv4_pass, **v_pass(1), start=False, stop=True)

        def let_through(i):
            gated[i] = keep.tile([P, J], F32, name="gated%d" % i)[:]
            nc.vector.tensor_tensor(out=gated[i], in0=values[i][:], in1=gates[i][:], op=MULT)

        def finish(a, b, engine, tag):
            t = keep.tile([P, b - a, J], F32, name="result%d" % a, tag=tag, align_bytes=64)
            for i in range(a, b):
                engine.tensor_tensor(out=t[:, i - a, :], in0=gated[i], in1=res_sb[i], op=ADD)
                if i == 3:
                    nc.sync.dma_start(out=dealt(out, 2, 4), in_=t[:, 2:4, :])
                elif i != 2:
                    nc.sync.dma_start(out=dealt(out, i, i + 1), in_=t[:, i - a:i - a + 1, :])

        load_weight(2, 0, 2, "table_words")
        load_weight(2, 2, PACK, "raw2")
        load_tiles(st, "st", 0, 1, st_sb)
        load_tiles(st, "st", 1, 2, st_sb)
        nc.sync.dma_start(out=wv4_raw[:], in_=wv4_words[0].bitcast(I32))
        load_tiles(st, "st", 2, 4, st_sb)
        load_tiles(res, "res", 0, 1, res_sb)
        load_tiles(st, "st", 4, 5, st_sb)
        load_tiles(res, "res", 1, 2, res_sb)
        load_tiles(st, "st", 5, 6, st_sb)
        load_tiles(res, "res", 2, 3, res_sb)
        load_tiles(st, "st", 6, 7, st_sb)
        load_tiles(st, "st", 7, 8, st_sb)
        load_tiles(res, "res", 3, 4, res_sb)
        load_tiles(res, "res", 4, 6, res_sb)
        load_tiles(res, "res", 6, 8, res_sb)
        prepare(0)
        prepare(1)
        for i in range(KEY_BANKS):
            key(i)
        for pair in range(PAIRS):
            interleave(2, 2 * pair * P, 2 * (pair + 1) * P, 0, 2, on_vector if pair < 3 else on_scalar)
        interleave(2, 0, 256, 2, PACK, on_vector)
        interleave(2, 256, 512, 2, PACK, on_scalar)
        interleave(2, 512, SPLIT, 2, PACK, on_vector)
        interleave(2, SPLIT, 768, 2, PACK, on_scalar)
        interleave(2, 768, N, 2, PACK, on_scalar)
        quantize(2, 0)
        quantize(2, 2)
        gate(0)
        quantize(2, 1)
        gate(1)
        quantize(2, 3)
        deal_wv4(PLAIN_PAIRS, PAIRS, "f1")
        for i in range(TILES):
            value(i)
            if KEY_BANKS <= i + 4 < TILES:
                key(i + 4)
            let_through(i)
            if i < 2:
                gate(i + 2)
            if 1 <= i < TILES - 3:
                gate(i + 3)
        finish(0, POOL_SUMS, nc.gpsimd, "grouped2_3")
        finish(POOL_SUMS, TILES, nc.vector, "late")
